import numpy as np, ml_dtypes
CORES = [2,42,66,74,82,90,114]
N = 7
BF = ml_dtypes.bfloat16
def gentries(a):
    return np.ascontiguousarray(a.reshape(8, 16, -1).transpose(0, 2, 1)).reshape(8, -1)
def gtable(e):
    e = np.asarray(e); return np.ascontiguousarray(e.reshape(8, -1, 16).transpose(0, 2, 1)).reshape(128, -1).astype(np.int32)
W, T, Z, VI, SH = 4096, 192, 5, 4, 5
STEP = (0, 1, 2, 4)
kk = np.arange(16)
def parts(rng):
    return rng.integers(0, 64, (N, 8, 16, W)), rng.integers(0, W, (N, 8, 4, T, 16)), rng.integers(450, 850, (N, 8, 16))
def pack(x, h, th):
    return {"x": np.ascontiguousarray(x.reshape(N, 128, W)).astype(np.float32).astype(BF), "hom": np.stack([gtable(a.reshape(8, -1)) for a in h]),
            "th": np.ascontiguousarray(th.reshape(N, 128, 1)).astype(np.int32)}
def lay(z, u, v):
    z, u, v = np.broadcast_arrays(z, u, v); s = np.arange(4)[:, None, None]
    return np.where((s == 0) | (s == z[..., None, :, :] + 1), u[..., None, :, :], v[..., None, :, :])
def setup_inputs(rng):
    return pack(*parts(rng))
def setup_inputs_spread(rng):
    x, h, th = parts(rng)
    x = (64 * np.exp2(-rng.integers(0, 7, (N, 8, 1, W))) * rng.random((N, 8, 16, W))).astype(np.int64)
    h = (W * rng.random((N, 8, 4, T, 16)) ** rng.integers(1, 5, (N, 8, 1, 1, 1))).astype(np.int64)
    th = (2017 * rng.random((N, 8, 16)) ** 3).astype(np.int64)
    return pack(x, np.minimum(h, W - 1), np.minimum(th, 2016))
def setup_inputs_ends(rng):
    x = 63 * rng.integers(0, 2, (N, 8, 16, W)); h = (W - 1) * rng.integers(0, 2, (N, 8, 4, T, 16)); th = 2016 * rng.integers(0, 2, (N, 8, 16))
    four = np.array([1, 2, W - 17, W - 2])
    for g in (0, 2, 4, 6, 7):
        e = 63 * rng.integers(0, 2, (N, 1)); x[:, g, :, 0] = e; x[:, g, :, W - 1] = 63 - e
        for j in range(4):
            x[:, g, :, int(four[j])] = np.where((j == 0) | (kk % 3 == j - 1), e, 63 - e)
    def zip3(j):
        return np.where(j < 3 * (Z // 3), j % 3, 3)
    a, b = kk < Z, kk >= 16 - Z
    top = np.where(a, zip3(kk), np.where(b, zip3(kk - 16 + Z), 1 + (kk & 1)))
    t2 = np.where(a, 0, np.where(b, 1, 2)); t3 = np.where(a, 2, np.where(b, 0, 1))
    late = np.where(b, 0, 2)
    turn = np.array([[0, 1, 2, 3], [0, 2, 1, 3], [0, 2, 3, 1]])
    def seq(z, j):
        return np.where((j == Z - 1) | (j % 3 == 0), z, np.where(j % 3 == 1, 0, 3 - z))
    def great(zl, zr, at):
        z = np.where(b, seq(zr, kk - 16 + Z), np.where(a, seq(zl, kk), zl))
        return np.where(a | b | (kk == at), four[turn[z]].T, lay(np.zeros((1, 16), np.int64), 0, W - 1)[:, 0])
    for g in (0, 7):
        for i, z in ((0, top), (1, late), (2, t3), (3, t2), (T - 5, t3), (T - 3, late), (T - 2, t2), (T - 1, top)):
            h[:, g, :, i] = lay(z[None, :], 0, W - 1)[:, 0]
        h[:, g, :, 4] = 0; h[:, g, :, T - 4] = W - 1
        for i, s in ((5, great(2, 1, 15 - Z)), (6, great(1, 2, Z)), (T - 7, great(1, 2, 15 - Z)), (T - 6, great(2, 1, Z))):
            h[:, g, :, i] = s
    th[:, ::2, 15] = 2016; th[:, 1::2, 15] = 0; th[:, ::2, 0] = 0; th[:, 1::2, 0] = 2016
    return pack(x, h, th)
def setup_inputs_corners(rng):
    x, h, th = parts(rng); own = 16 * np.arange(T)[:, None] + kk
    th = rng.choice(np.array([0, 1, 31, 600, 700, 2015, 2016]), (N, 8, 16))
    for q in range(N):
        for g in range(8):
            c = (q + g) % 8
            if c == 0: h[q, g] = 0
            if c == 1: h[q, g] = W - 1
            if c == 2: h[q, g] = own
            if c == 3: h[q, g, 0] = own; h[q, g, 1] = W - 1 - own; h[q, g, 2] = 0; h[q, g, 3] = W - 1
            if c == 4: h[q, g] = h[q, g, 0].copy()
            if c == 5: h[q, g] = rng.choice(np.array([Z, 16 * (T - 1) + 16 - Z, 0, W - 1]), (4, T, 16))
            if c == 6: h[q, g, :, ::2] = 0
            if c == 7: h[q, g, :, 1::2] = rng.choice(W - np.array([3, 5, 7, 9, 19, 21]), (4, T // 2, 16)); th[q, g] = rng.choice(np.array([0, 1, 31]), 16)
    return pack(x, h, th)
def setup_inputs_crowd(rng):
    x, h, th = parts(rng)
    x[:, :, 0] = (x[:, :, 0] & 62) | (np.arange(W) & 1); x[..., 2::4] = x[..., 0::4]; x[..., 3::4] = x[..., 1::4]
    p = rng.integers(0, 3, (N, 8, T)); q = (p + rng.integers(1, 3, (N, 8, T))) % 3
    n = np.array([T, T - 1, 0, 1, 31, 32, T // 2, T - 32])[(np.arange(8)[None, :] + np.arange(N)[:, None]) % 8]
    n[N - 1] = np.array([T, T - 1, T, T - 1, T - 1, T - 1, T - 1, T])
    q = np.where(np.argsort(rng.random((N, 8, T)), axis=-1) < n[..., None], q, p)
    at = rng.integers(Z, 17 - Z, (N, 8, T)); at[..., 0] = Z; at[..., T - 1] = 16 - Z
    u = 2 * rng.integers(0, W // 2, (N, 8, T, 16)); v = 2 * rng.integers(0, W // 2, (N, 8, T, 16)) + 1
    h = lay(np.where(kk < at[..., None], p[..., None], q[..., None]), u, v) ^ (2 * rng.integers(0, 2, (N, 8, 4, T, 16)))
    return pack(x, h, th)
def setup_inputs_ties(rng):
    x, h, th = parts(rng); top = rng.integers(1, 4, (N, 8, 1, 1)); top[:, 7] = 1; top[:, 0] = 3
    x = np.minimum((rng.random((N, 8, 16, W)) * (top + 1)).astype(np.int64), top)
    h[:, ::2, :, ::2] = lay(rng.integers(0, 4, (N, 4, T // 2, 16)), rng.integers(0, W, (N, 4, T // 2, 16)), rng.integers(0, W, (N, 4, T // 2, 16)))
    return pack(x, h, rng.integers(0, 21, (N, 8, 16)))
def check_inputs(d):
    bad = []
    for k, lo, hi in (("x", 0, 63), ("hom", 0, W - 1), ("th", 0, 2016)):
        a = np.asarray(d[k]).astype(np.float64)
        if not (np.min(a) >= lo and np.max(a) <= hi): bad.append("range of " + k)
        elif np.any(a != np.floor(a)): bad.append("whole numbers in " + k)
    return bad
def reference(x, hom, th):
    v = x.astype(np.float32).astype(np.int32).reshape(N, 8, 16, W)
    s = np.stack([gentries(a) for a in hom]).astype(np.int64).reshape(N, 8, 4, T, 16)
    t = th.astype(np.int64).reshape(N, 8, 1, 16); A = np.zeros((N, 8), np.int64)
    strand = np.arange(4)[None, None, :, None, None]
    for visit in range(VI):
        p = [np.take_along_axis(v, s[:, :, a].reshape(N, 8, 1, 16 * T), 3) for a in range(4)]
        def dist(a, b):
            return np.add.reduce(np.abs(p[a] - p[b]), axis=2).reshape(N, 8, T, 16).astype(np.int64)
        c = np.stack([dist(0, 1) + dist(2, 3), dist(0, 2) + dist(1, 3), dist(0, 3) + dist(1, 2)])
        L = np.argmin(np.add.reduce(c[..., :Z], axis=-1), axis=0); R = np.argmin(np.add.reduce(c[..., 16 - Z:], axis=-1), axis=0)
        cl = np.take_along_axis(c, L[None, ..., None], 0)[0]; cr = np.take_along_axis(c, R[None, ..., None], 0)[0]
        tot = np.stack([np.add.reduce(cl[..., :m], axis=-1) + np.add.reduce(cr[..., m:], axis=-1) for m in range(Z, 17 - Z)])
        meet = Z + np.argmin(tot, axis=0)
        right = kk >= meet[..., None]
        over = np.where(right, cr, cl) > t + (A & 31)[:, :, None, None]
        mate = strand ^ (np.where(right, R[..., None], L[..., None])[:, :, None] + 1)
        new = ((s * np.take_along_axis(s, mate, 2) >> SH) + s + 37 * kk) & (W - 1)
        s = np.where(over[:, :, None] & (mate < strand), new, s)
        sw = L != R
        s = np.where((sw[..., None] & right)[:, :, None], np.take_along_axis(s, mate, 2), s)
        at = (kk == meet[..., None]).reshape(N, 8, 1, 16 * T)
        v[..., :16 * T] = np.where(at, (v[..., :16 * T] + p[0]) >> 1, v[..., :16 * T])
        A = np.add.reduce(sw.astype(np.int64), axis=-1)
        s = np.stack([np.roll(s[:, :, a], STEP[a], axis=0) for a in range(4)], axis=2)
    return {"yx": v.reshape(N, 128, W).astype(np.float32).astype(BF), "ys": np.stack([gtable(a.reshape(8, -1)) for a in s]).astype(np.float32)}

@@ -1,0 +1,540 @@
+from concourse.bass import DstId, RemoteDMATransfer
+from concourse.mybir import AluOpType as A, ActivationFunctionType as F
+
+VI = 4
+NC = 3
+HALF = 512
+STEP = (0, 1, 2, 4)
+PAIRS = ("02", "23", "03", "13", "01", "12")
+GORDER = ((2, 0), (0, 0), (2, 1), (0, 1), (3, 0), (3, 1), (1, 0), (1, 1))
+
+CY, PEC, GAM, SCA, WAKE, NET = 1.0, 0.5, 1.8, 4.5, 70.0, 4000.0
+
+SCRATCH = {"xs": ("sbuf", [128, 4096], "bfloat16"), "homi": ("sbuf", [128, 768], "int32"), "lists": ("sbuf", [128, 12], "uint16"),
+           "thi": ("sbuf", [128, 1], "int32"), "ysb": ("sbuf", [128, 768], "float32"), "ici": ("sbuf", [128, 8], "int32"),
+           "ip": ("sbuf", [128, 1], "int32"), "accb": ("sbuf", [128, 4], "bfloat16")}
+PLACE = {}
+for _v in range(VI):
+    SCRATCH["off%d" % _v] = ("sbuf", [128, 768], "uint16")
+    SCRATCH["snd%d" % _v] = ("sbuf", [128, 576], "uint16" if _v < VI - 1 else "float32")
+for _s in range(4):
+    SCRATCH["g%d" % _s] = ("sbuf", [128, 3072], "bfloat16")
+for _b in range(8):
+    SCRATCH["pb%d" % _b] = ("psum", [128, 512], "float32")
+for _p in range(2):
+    for _n in PAIRS:
+        SCRATCH["d%s_%d" % (_n, _p)] = ("sbuf", [128, 1024], "bfloat16")
+
+
+def _pack(buf, dtype, names):
+    at = 0
+    for n, w in names:
+        PLACE[n] = (buf, at, w)
+        at += (w + 15) // 16 * 16
+    SCRATCH[buf] = ("sbuf", [128, at], dtype)
+
+
+for _p in range(NC):
+    for _k, _d, _l in (("h", "float16", (("ab", 128), ("c1", 64), ("y", 128), ("zz", 128), ("fs", 256), ("src", 192), ("vv", 64), ("ps", 256), ("st", 256))),
+                       ("b", "bfloat16", (("u", 64), ("o", 64), ("tu", 128), ("om", 64), ("gs", 64), ("ts", 64), ("same", 64), ("xr", 320), ("fb", 128),
+                                          ("tq", 64))),
+                       ("f", "float32", (("m1", 64), ("lt", 32), ("sr", 128), ("gd", 128))),
+                       ("i", "int32", (("pp", 128), ("qq", 128), ("zi", 128), ("ui", 128), ("nb", 128)))):
+        _pack("w%s%d" % (_k, _p), _d, [("%s_%d" % (_n, _p), _w) for _n, _w in _l])
+_pack("conh", "float16", [(_n, 128) for _n in ("idh", "ndh", "d37", "wza", "wzb", "wta", "wtb")])
+_pack("conb", "bfloat16", [(_n, 128) for _n in ("idb", "onb", "wc", "ca", "cb", "wr", "wrn", "wp2", "wsn", "wl0", "wl2", "bl0", "bl2", "br0", "br2", "b2k",
+                                                "rw")] + [("red", 144), ("reds", 144), ("ale", 131), ("alo", 131), ("m192", 64)])
+_pack("conf", "float32", [("ia", 144), ("onf", 128), ("nof", 128), ("idf", 128), ("ndf", 128), ("bm", 128), ("bm0", 128), ("jj", 128), ("kc", 1), ("ek", 16),
+                          ("acc", 4), ("thf", 2), ("j17", 17)] + [("t%d" % _n, 128) for _n in range(4)] + [("f%d" % _n, 17) for _n in range(8)] +
+      [("q%d" % _n, 17) for _n in range(4)] + [("col%d" % _n, 1) for _n in range(40)])
+SEMAPHORES = ["s_pe", "s_dve", "s_act", "s_pool", "sent", "dx", "dh", "dt", "dy0", "dy1", "dy2", "dy3", "dys"]
+SEMAPHORES += ["arr%d_%d" % (_v, _c) for _v in range(VI) for _c in range(NC)]
+CACHE = {}
+
+
+def schedule(nodes):
+    n = len(nodes)
+    succ = [[] for _ in range(n)]
+    for i, x in enumerate(nodes):
+        for d in x["deps"] | x["odeps"]:
+            succ[d].append(i)
+    level = [0.0] * n
+    for i in range(n - 1, -1, -1):
+        x = nodes[i]
+        level[i] = x["cost"] + x["lat"] + max([level[j] + (WAKE if i in nodes[j]["deps"] else 0.0) for j in succ[i]] + [0.0])
+    left = [len(x["deps"] | x["odeps"]) for x in nodes]
+    ready = [0.0] * n
+    free, cand, order = {}, {}, []
+    for i, x in enumerate(nodes):
+        if left[i] == 0:
+            cand.setdefault(x["q"], []).append(i)
+    while len(order) < n:
+        best = None
+        for q, l in cand.items():
+            if not l:
+                continue
+            t = free.get(q, 0.0) if q is not None else 0.0
+            first = max(t, min(ready[i] for i in l))
+            i = max((i for i in l if ready[i] <= first + 1.0), key=lambda i: (level[i], -i))
+            if best is None or max(first, ready[i]) < best[0]:
+                best = (max(first, ready[i]), q, i)
+        s, q, i = best
+        cand[q].remove(i)
+        order.append(i)
+        x = nodes[i]
+        free[q] = s + x["cost"]
+        end = s + x["cost"] + x["lat"]
+        for j in succ[i]:
+            e = end + WAKE if i in nodes[j]["deps"] else s + x["cost"]
+            ready[j] = max(ready[j], e)
+            left[j] -= 1
+            if left[j] == 0:
+                cand.setdefault(nodes[j]["q"], []).append(j)
+    return order
+
+
+def rank_program(g, core, T, topo):
+    rank = T.rank_of(core)
+    if rank is None:
+        return
+    Q = {"pe": g.tensor, "dve": g.vector, "act": g.scalar, "pool": g, "sp": g.sync}
+    nodes, lastw, readers, banks = [], {}, {}, {}
+    pb = [T["pb%d" % b] for b in range(8)]
+
+    def B(name, lo=0, hi=None, st=1):
+        buf, at, w = PLACE[name]
+        hi = w if hi is None else hi
+        return T[buf][:, at + lo:at + hi:st] if st > 1 else T[buf][:, at + lo:at + hi]
+
+    def op(q, fns, cost, r=(), w=(), b=(), ext=None, lat=0.0):
+        i = len(nodes)
+        deps, odeps = set(), set()
+        for t in r:
+            if t in lastw:
+                deps.add(lastw[t])
+        for t in w:
+            if t in lastw:
+                deps.add(lastw[t])
+            deps |= readers.get(t, set())
+        for t in b:
+            for q2, d in banks.get(t, {}).items():
+                (odeps if q2 == q else deps).add(d)
+        nodes.append({"q": q, "fns": fns, "cost": cost, "deps": deps, "odeps": odeps - deps, "ext": ext, "lat": lat})
+        for t in r:
+            readers.setdefault(t, set()).add(i)
+        for t in w:
+            lastw[t] = i
+            readers[t] = set()
+        for t in b:
+            banks.setdefault(t, {})[q] = i
+        return i
+
+    def tt(n, out, in0, in1, o, r=(), w=(), b=(), cost=None):
+        op("dve", [lambda: g.vector.tensor_tensor(out=out, in0=in0, in1=in1, op=o)], cost or CY * max(64, n * (1 if b else 2)), r, w, b)
+
+    def ts(n, out, in0, s1, o0, s2=None, o1=None, r=(), w=(), b=()):
+        if o1 is None:
+            op("dve", [lambda: g.vector.tensor_scalar(out=out, in0=in0, scalar1=s1, scalar2=None, op0=o0)], CY * max(64, n), r, w, b)
+        else:
+            op("dve", [lambda: g.vector.tensor_scalar(out=out, in0=in0, scalar1=s1, scalar2=s2, op0=o0, op1=o1)], CY * max(64, n), r, w, b)
+
+    def cp(n, out, in_, r=(), w=(), b=(), cost=None):
+        op("dve", [lambda: g.vector.tensor_copy(out=out, in_=in_)], cost or CY * max(64, n), r, w, b)
+
+    def act(n, out, in_, func, bias=0.0, accum=None, r=(), w=(), b=(), cost=None):
+        if accum is None:
+            op("act", [lambda: g.scalar.activation(out=out, in_=in_, func=func, bias=bias)], cost or CY * max(64, n), r, w, b)
+        else:
+            op("act", [lambda: g.scalar.activation(out=out, in_=in_, func=func, bias=bias, accum_out=accum)], cost or CY * max(64, n), r, w, b)
+
+    def mms(bank, lo, hi, terms, start=True, stop=True):
+        def one(l, x, s, e):
+            return lambda: g.tensor.matmul(out=pb[bank][:, lo:hi], lhsT=l, rhs=x, start=s, stop=e)
+        fns = [one(x[0], x[1], start and j == 0, stop and j == len(terms) - 1) for j, x in enumerate(terms)]
+        cost = sum(PEC * max(64, hi - lo) * (x[3] if len(x) > 3 else 1) for x in terms)
+        op("pe", fns, cost, tuple({t for x in terms for t in x[2]}), (), (bank,))
+
+    def dma(q, eng, out, in_, sem, r=(), w=(), lat=2500.0):
+        op(q, [lambda: eng.dma_start(out=out, in_=in_)], 60.0, r, w, ext=(sem, 16), lat=lat)
+
+    dma("sp", g.sync, T.homi[:], T.hom[:], "dh", (), ("homi",), 3500.0)
+    dma("sp", g.sync, T.xs[:], T.x[:], "dx", (), ("x0", "x1", "x2", "x3"), 6500.0)
+    dma("act", g.scalar, T.thi[:], T.th[:], "dt", (), ("thi",))
+
+    def iota(out, pattern, base, cm, w, n, flag=True):
+        if flag:
+            op("pool", [lambda: g.iota(out, pattern, base, cm, allow_small_or_imprecise_dtypes=True)], 160 + 2 * n, (), (w,))
+        else:
+            op("pool", [lambda: g.iota(out, pattern, base, cm)], 160 + 2 * n, (), (w,))
+
+    def sel(out, in_, pattern, o, base, cm, r, w):
+        op("pool", [lambda: g.affine_select(out, in_, pattern, o, 0.0, base, cm)], 480, r, (w,))
+
+    def fill(name, x):
+        op("dve", [lambda: g.vector.memset(B(name), x)], 128, (), (name,))
+    iota(T.ip[:], [[0, 1]], 0, 1, "ip", 1, False)
+    iota(B("ia"), [[1, 144]], 0, 0, "ia", 144)
+    fill("onb", 1.0)
+    fill("onf", 1.0)
+    fill("nof", -1.0)
+    fill("m192", -192.0)
+    EYE = [[-1, 128]]
+    sel(B("idb"), B("onb"), EYE, A.is_equal, 0, 1, ("onb",), "idb")
+    iota(B("jj"), [[0, 8], [1, 16]], 0, 0, "jj", 128)
+    sel(B("bm0"), B("onf"), [[-16, 8], [0, 16]], A.is_ge, 0, 1, ("onf",), "bm0")
+    sel(B("bm"), B("bm0"), [[16, 8], [0, 16]], A.is_ge, 15, -1, ("bm0",), "bm")
+    sel(B("idf"), B("onf"), EYE, A.is_equal, 0, 1, ("onf",), "idf")
+    sel(B("ndf"), B("nof"), EYE, A.is_equal, 0, 1, ("nof",), "ndf")
+    iota(B("rw"), [[0, 4], [256, 32]], 0, 0, "rw", 128)
+    ncol = [0]
+
+    def col(n, in_, s1, o0, s2=None, o1=None, r=()):
+        name = "col%d" % ncol[0]
+        ncol[0] += 1
+        ts(n, B(name), in_, s1, o0, s2, o1, r=r, w=(name,))
+        return B(name), name
+    ici = T.ici
+    ts(1, ici[:, 0:1], T.ip[:], 15, A.bitwise_and, r=("ip",), w=("i0",))
+    ts(1, ici[:, 1:2], T.ip[:], 31, A.bitwise_and, r=("ip",), w=("i1",))
+    ts(1, ici[:, 2:3], T.ip[:], 16, A.bitwise_and, r=("ip",), w=("i2",))
+    pc, pct = col(1, T.ip[:], 0.0, A.add, r=("ip",))
+    kc, kct = B("kc"), "kc"
+    cp(1, kc, ici[:, 0:1], r=("i0",), w=(kct,))
+    tgb, tgbt = col(1, kc, -1.0, A.mult, pc, A.add, r=(kct, pct))
+    tgc, tgct = col(1, tgb, 15.0, A.add, r=(tgbt,))
+    ts(144, B("red"), B("ia"), tgc, A.is_equal, 2.0, A.mult, r=("ia", tgct), w=("red",))
+    ts(144, B("reds"), B("ia"), tgc, A.is_equal, r=("ia", tgct), w=("reds",))
+    ts(128, B("t0"), B("bm"), -512.0, A.mult, 512.0, A.add, r=("bm",), w=("t0",))
+    tt(128, B("jj"), B("jj"), B("t0"), A.add, r=("jj", "t0"), w=("jj",))
+    ts(16, B("ek"), B("ia", 0, 16), kc, A.is_equal, r=("ia", kct), w=("ek",))
+    cp(16, B("j17", 0, 16), B("ia", 0, 16), r=("ia",), w=("j17",))
+    cp(1, B("j17", 16, 17), kc, r=(kct,), w=("j17k",))
+    JT = ("j17", "j17k")
+
+    def fn(dst, start, steps):
+        for q, (co, t) in enumerate(steps):
+            tmp = "q%d" % (q % 4)
+            ts(17, B(tmp), B("j17"), float(t), A.is_ge, float(co), A.mult, r=JT, w=(tmp,))
+            if q == 0 and start is None:
+                tt(17, B(dst), B("j17"), B(tmp), A.add, r=JT + (tmp,), w=(dst,))
+            elif q == 0:
+                ts(17, B(dst), B(tmp), float(start), A.add, r=(tmp,), w=(dst,))
+            else:
+                tt(17, B(dst), B(dst), B(tmp), A.add, r=(tmp, dst), w=(dst,))
+
+    def both(name, out, n, in0, s1, o1, in1, s2, o2, mix, r):
+        ts(n, B("t0", 0, n), in0, s1, o1, r=r, w=("t0",))
+        ts(n, B("t1", 0, n), in1, s2, o2, r=r, w=("t1",))
+        tt(n, out, B("t0", 0, n), B("t1", 0, n), mix, r=("t0", "t1"), w=(name,))
+
+    def signs(name, p, m):
+        both(name, B(name), 128, B("jj"), B(p, 16, 17), A.is_equal, B("jj"), B(m, 16, 17), A.is_equal, A.subtract, ("jj", p, m))
+
+    def window(name, p, m):
+        both("t2", B("t2", 0, 16), 16, B(p, 0, 16), kc, A.is_le, B(m, 0, 16), kc, A.is_gt, A.mult, (p, m, kct))
+        for q in range(8):
+            ts(16, B(name, 16 * q, 16 * q + 16), B("t2", 0, 16), B("bm", 16 * q, 16 * q + 1), A.mult, r=("t2", "bm"), w=(name if q == 7 else name + str(q),))
+    r5, r5t = col(1, kc, 5.0, A.is_ge, 9000.0, A.mult, r=(kct,))
+    zl, zlt = col(1, kc, 11.0, A.is_ge, -8997.0, A.mult, r=(kct,))
+    lo, lot = col(1, r5, zl, A.add, r=(r5t, zlt))
+    l1, l1t = col(1, lo, 1.0, A.add, r=(lot,))
+    l2, l2t = col(1, lo, 2.0, A.add, r=(lot,))
+    ts(128, B("t3"), B("jj"), l1, A.is_le, r=("jj", l1t), w=("t3",))
+    ts(128, B("t2"), B("jj"), lo, A.is_ge, -1.0, A.mult, r=("jj", lot), w=("t2",))
+    tt(128, B("wza"), B("t2"), B("t3"), A.mult, r=("t2", "t3"), w=("wza",))
+    both("wzb", B("wzb"), 128, B("jj"), l1, A.is_ge, B("jj"), l2, A.is_le, A.mult, ("jj", l1t, l2t))
+
+    def spread(name, terms):
+        c = ct = None
+        for co, t in terms:
+            if c is None:
+                c, ct = col(1, B("ek", t, t + 1), float(co), A.mult, r=("ek",))
+            else:
+                c, ct = col(1, B("ek", t, t + 1), float(co), A.mult, c, A.add, r=("ek", ct))
+        ts(128, B(name), B("bm"), c, A.mult, r=("bm", ct), w=(name,))
+    fn("f0", 0.0, ((1, 2), (2, 3), (1, 5), (99, 6)))
+    fn("f1", 1.0, ((1, 1), (2, 3), (1, 4), (99, 6)))
+    signs("wc", "f0", "f1")
+    ts(8, B("wc", 15, 128, 16), B("bm", 15, 128, 16), B("ek", 15, 16), A.mult, 2.0, A.mult, r=("bm", "ek", "wc"), w=("wc",))
+    spread("wl0", ((1, 0), (-1, 3)))
+    spread("wl2", ((1, 2), (-1, 5)))
+    for wname, cname, a0, p, m in (("wta", "ca", (5, 7), ((-5, 5), (-6, 11), (99, 15)), ((-6, 5), (-4, 11), (99, 15))),
+                                   ("wtb", "cb", (99, 103), ((-99, 5), (-3, 8), (-2, 10), (99, 11)), ((-99, 5), (-2, 8), (-1, 10), (99, 11)))):
+        for q, (dst, steps) in enumerate((("f2", p), ("f3", m))):
+            fn(dst, None, steps)
+            ts(17, B(dst), B(dst), float(a0[q]), A.add, r=(dst,), w=(dst,))
+        window(wname, "f2", "f3")
+        signs(cname, "f2", "f3")
+    tE, tEt = col(1, ici[:, 2:3], 999.0, A.mult, r=("i2",))
+    ta, tat = col(1, ici[:, 1:2], -1.0, A.mult, pc, A.add, r=("i1", pct))
+    te, tet = col(1, ta, tE, A.add, 3.0, A.add, r=(tat, tEt))
+    to, tot = col(1, tE, -1.0, A.mult, ta, A.add, r=(tEt, tat))
+    to, tot = col(1, to, 16 * 999.0 + 3.0, A.add, r=(tot,))
+    ts(131, B("ale"), B("ia", 0, 131), te, A.is_equal, kc, A.mult, r=("ia", tet, kct), w=("ale",))
+    ts(131, B("alo"), B("ia", 0, 131), to, A.is_equal, kc, A.mult, r=("ia", tot, kct), w=("alo",))
+    k16, k16t = col(1, kc, 16.0, A.mult, r=(kct,))
+    cp(128, B("idh"), B("idf"), r=("idf",), w=("idh",))
+    cp(128, B("ndh"), B("ndf"), r=("ndf",), w=("ndh",))
+    k37, k37t = col(1, kc, 37.0, A.mult, r=(kct,))
+    ts(128, B("d37"), B("idf"), k37, A.mult, r=("idf", k37t), w=("d37",))
+    both("wr", B("wr"), 128, B("jj"), kc, A.is_ge, B("bm"), 1.0, A.mult, A.mult, ("jj", kct, "bm"))
+    ts(128, B("wrn"), B("wr"), -1.0, A.mult, r=("wr",), w=("wrn",))
+    fn("f4", None, ((-3, 3), (99, 6)))
+    ts(128, B("wp2"), B("jj"), B("f4", 16, 17), A.is_equal, r=("jj", "f4"), w=("wp2",))
+    spread("wsn", ((-1, 0), (-1, 1), (-1, 2)))
+    spread("bl0", ((1, 0),))
+    spread("bl2", ((1, 2),))
+    spread("br0", ((1, 3), (-1, 15)))
+    spread("br2", ((1, 5), (-1, 15)))
+    spread("b2k", ((2048, 15),))
+    cp(1, B("thf", 0, 1), T.thi[:], r=("thi",), w=("thf0",))
+
+    for c in range(NC):
+        for s in (2, 0, 3, 1):
+            cp(64, T.off0[:, c * 256 + s * 64:c * 256 + s * 64 + 64], T.homi[:, s * 192 + c * 64:s * 192 + c * 64 + 64], r=("homi",), w=("off0_%d_%d" % (c, s),))
+
+    def gather(v, c, s, h):
+        lo = c * 256 + s * 64 + h * 32
+        at = c * 1024 + h * HALF
+        act(0, T["g%d" % s][:, at:at + HALF], T.xs[:, 0:4096].indirect(T["off%d" % v][:, lo:lo + 32]), F.Copy,
+            r=("x0", "x1", "x2", "x3", "off%d_%d_%d" % (v, c, s)), w=("g%d_%d_%d" % (s, c, h),), cost=70 + GAM * HALF)
+    uc = [0]
+
+    def ufill(c, s, h):
+        bank = uc[0] % 4
+        uc[0] += 1
+        at = c * 1024 + h * HALF
+        mms(bank, 0, 512, [(B("idb"), T["g%d" % s][:, at:at + HALF], ("idb", "g%d_%d_%d" % (s, c, h)))])
+        return bank
+
+    def pair(c, par, s, bank, name, h):
+        at = c * 1024 + h * HALF
+        tt(HALF, T["d%s_%d" % (name, par)][:, h * HALF:h * HALF + HALF], T["g%d" % s][:, at:at + HALF], pb[bank][:, 0:512], A.max,
+           r=("g%d_%d_%d" % (s, c, h),), w=("d%s_%d_%d" % (name, par, h),), b=(bank,))
+
+    def red(par, name, bank, at, first, last):
+        d = T["d%s_%d" % (name, par)]
+        toks = ("red", "d%s_%d_0" % (name, par), "d%s_%d_1" % (name, par))
+        for q in range(2):
+            mms(bank, at, at + 64, [(B("red", 15 - k, 143 - k), d[:, k:1024:16], toks) for k in range(8 * q, 8 * q + 8)],
+                first and q == 0, last and q == 1)
+
+    def total(c):
+        for q, s in enumerate((2, 0, 3, 1)):
+            for e in range(2):
+                mms(5, 64, 128, [(B("reds", 15 - k, 143 - k), T["g%d" % s][:, c * 1024 + k:c * 1024 + 1024:16],
+                                  ("reds", "g%d_%d_0" % (s, c), "g%d_%d_1" % (s, c))) for k in range(8 * e, 8 * e + 8)], q == 0 and e == 0, q == 3 and e == 1)
+
+    def main(v, c):
+        par = (v * NC + c) % 2
+        u2 = [ufill(c, 2, 0), ufill(c, 2, 1)]
+        pair(c, par, 0, u2[0], "02", 0)
+        pair(c, par, 0, u2[1], "02", 1)
+        u3 = [ufill(c, 3, 0), ufill(c, 3, 1)]
+        red(par, "02", 4, 0, True, False)
+        pair(c, par, 3, u2[0], "23", 0)
+        pair(c, par, 3, u2[1], "23", 1)
+        u1 = [ufill(c, 1, 0), ufill(c, 1, 1)]
+        red(par, "23", 5, 0, True, False)
+        pair(c, par, 0, u3[0], "03", 0)
+        pair(c, par, 0, u3[1], "03", 1)
+        pair(c, par, 1, u3[0], "13", 0)
+        pair(c, par, 1, u3[1], "13", 1)
+        red(par, "13", 4, 0, False, True)
+        pair(c, par, 0, u1[0], "01", 0)
+        pair(c, par, 0, u1[1], "01", 1)
+        red(par, "01", 5, 0, False, True)
+        m1 = "m1_%d" % c
+        cp(64, B(m1), pb[4][:, 0:64], w=(m1,), b=(4,))
+        red(par, "03", 4, 64, True, False)
+        tt(64, B("ab_%d" % c, 0, 64), pb[5][:, 0:64], B(m1), A.subtract, r=(m1,), w=("a_%d" % c,), b=(5,))
+        pair(c, par, 2, u1[0], "12", 0)
+        pair(c, par, 2, u1[1], "12", 1)
+        red(par, "12", 4, 64, False, True)
+        tt(64, B("ab_%d" % c, 64, 128), pb[4][:, 64:128], B(m1), A.subtract, r=(m1,), w=("b_%d" % c,), b=(4,))
+        total(c)
+        tt(64, B("c1_%d" % c), B(m1), pb[5][:, 64:128], A.subtract, r=(m1,), w=("c1_%d" % c,), b=(5,))
+
+    def crit(v, c):
+        bk = 6
+        n = lambda s: "%s_%d" % (s, c)
+        mms(bk, 0, 64, [(B("wza"), B(n("ab"), 0, 64), ("wza", n("a"))), (B("wzb"), B(n("ab"), 64, 128), ("wzb", n("b")))])
+        act(64, B(n("u")), pb[bk][:, 0:64], F.Sign, 0.5, w=(n("u"),), b=(bk,))
+        mms(bk, 64, 128, [(B("wc"), B(n("u")), ("wc", n("u")))])
+        act(64, B(n("o")), pb[bk][:, 64:128], F.Relu, -1.0, w=(n("o"),), b=(bk,))
+        mms(bk, 128, 192, [(B("wl0"), B(n("o")), ("wl0", n("o")))])
+        mms(bk, 192, 256, [(B("wl2"), B(n("o")), ("wl2", n("o")))])
+        tt(128, B(n("y")), B(n("ab")), pb[bk][:, 128:256], A.mult, r=(n("a"), n("b")), w=(n("y"),), b=(bk,))
+        for q, m in enumerate(("wta", "wtb")):
+            mt = tuple([m] + [m + str(e) for e in range(7)])
+            mms(bk, 256 + 64 * q, 320 + 64 * q, [(B(m), B(n("y"), 0, 64), mt + (n("y"),)), (B(m), B(n("y"), 64, 128), mt + (n("y"),))])
+        act(128, B(n("tu")), pb[bk][:, 256:384], F.Sign, 0.5, w=(n("tu"),), b=(bk,))
+        mms(bk, 384, 448, [(B("ca"), B(n("tu"), 0, 64), ("ca", n("tu"))), (B("cb"), B(n("tu"), 64, 128), ("cb", n("tu")))])
+        act(64, B(n("om")), pb[bk][:, 384:448], F.Relu, -5.0, w=(n("om"),), b=(bk,))
+        for q, m in enumerate(("ale", "alo")):
+            mms(bk, 448 + 16 * q, 464 + 16 * q, [(B("rw")[0:1, :], B("onb", 0, 16)[0:1, :], ("rw", "onb"))] +
+                [(B(m, 3 - r, 131 - r), B(n("om"), 16 * r, 16 * r + 16), (m, n("om"))) for r in range(4)])
+        op("dve", [lambda: g.vector.transpose(out=B(n("lt")), in_=pb[bk][:, 448:480])], 64, (), (n("lt"),), (bk,))
+        li, lit = T.lists[:, 4 * c:4 * c + 4], n("li")
+        ts(4, li, B(n("lt"), 0, 4), k16, A.add, r=(n("lt"), k16t), w=(lit,))
+        cp(64, B(n("gs")), T.g0[:, c * 1024:c * 1024 + 1024].indirect(li), r=(lit, "g0_%d_0" % c, "g0_%d_1" % c), w=(n("gs"),), cost=60 + 64 * GAM)
+        tt(64, B(n("ts")), T.xs[:, c * 1024:c * 1024 + 1024].indirect(li), B(n("gs")), A.add, r=(lit, n("gs"), "x%d" % c), w=(n("ts"),), cost=60 + 64 * GAM)
+        ts(64, B(n("tq")), B(n("ts")), 0.5, A.mult, 191.75, A.add, r=(n("ts"),), w=(n("tq"),))
+
+    def scatter(c):
+        tt(64, T.xs[:, c * 1024:c * 1024 + 1024].indirect(T.lists[:, 4 * c:4 * c + 4]), B("tq_%d" % c), B("m192"), A.add,
+           r=("tq_%d" % c, "m192", "li_%d" % c), w=("x%d" % c,), cost=60 + 64 * SCA)
+
+    def upd(v, c):
+        bk = 7
+        n = lambda s: "%s_%d" % (s, c)
+        st, stt = B(n("st")), n("st")
+        i16, n16, ib = B("idh"), B("ndh"), B("idb")
+        ts(256, st, T["off%d" % v][:, c * 256:c * 256 + 256], -2048.0, A.add, r=tuple("off%d_%d_%d" % (v, c, s) for s in range(4)), w=(stt,))
+        mms(bk, 448, 512, [(B("wp2"), B(n("o")), ("wp2", n("o")))])
+        act(64, B(n("same")), pb[bk][:, 448:512], F.Relu, -1.0, accum=B("acc", c, c + 1), w=(n("same"), "acc%d" % c), b=(bk,))
+        o, om = B(n("o")), B(n("om"))
+        for q, (m, w) in enumerate((("bl0", "wrn"), ("br0", "wr"), ("bl2", "wrn"), ("br2", "wr"))):
+            mms(bk, 64 * q, 64 * q + 64, [(B(m), o, (m, n("o"))), (B(w), om, (w, n("om")))])
+        mms(bk, 256, 320, [(B("wr"), om, ("wr", n("om"))), (B("wsn"), B(n("same")), ("wsn", n("same")))])
+        xr = n("xr")
+        act(320, B(xr), pb[bk][:, 0:320], F.Relu, w=(xr,), b=(bk,))
+        for q in range(4):
+            a = q // 2 * 128
+            mms(bk, 64 * q, 64 * q + 64, [(ib, B(xr, a, a + 64), ("idb", xr)), (ib, B(xr, a + 64, a + 128), ("idb", xr))])
+        fs = n("fs")
+        tt(128, B(fs, 0, 128), B(stt, 64, 192), pb[bk][:, 0:128], A.mult, r=(stt,), w=(fs,), b=(bk,))
+        tt(128, B(fs, 128, 256), B(stt, 128, 256), pb[bk][:, 128:256], A.mult, r=(stt,), w=(fs + "x",), b=(bk,))
+        tt(128, B(n("zz")), B(n("ab")), pb[bk][:, 64:192], A.mult, r=(n("a"), n("b")), w=(n("zz"),), b=(bk,))
+        act(128, B(n("fb")), pb[bk][:, 64:192], F.Copy, w=(n("fb"),), b=(bk,))
+        f1, f2, h2, h3 = B(fs, 0, 64), B(fs, 64, 128), B(fs, 128, 192), B(fs, 192, 256)
+        s0, s1, s2, s3 = [B(stt, 64 * q, 64 * q + 64) for q in range(4)]
+        FT = ("idh", "ndh", stt, fs, fs + "x")
+        mms(bk, 256, 320, [(i16, s0, FT)])
+        mms(bk, 320, 384, [(i16, s1, FT), (n16, f1, FT), (i16, f2, FT)])
+        mms(bk, 384, 448, [(i16, B(n("c1")), ("idh", n("c1"))), (i16, B(n("zz"), 0, 64), ("idh", n("zz"))), (i16, B(n("zz"), 64, 128), ("idh", n("zz")))])
+        act(128, B(n("sr")), pb[bk][:, 256:384], F.Identity, 2048.0, w=(n("sr"),), b=(bk,))
+        ts(64, B(n("vv")), pb[bk][:, 384:448], B("thf", v % 2, v % 2 + 1), A.is_gt, r=("thf%d" % (v % 2),), w=(n("vv"),), b=(bk,))
+        cp(64, B(n("src"), 0, 64), pb[bk][:, 320:384], w=(n("src"),), b=(bk,))
+        k2 = (B("b2k"), o, ("b2k", n("o")))
+        qt = [(i16, s2, FT), (i16, f1, FT), (n16, f2, FT), (i16, h3, FT), (n16, h2, FT), k2]
+        tq = [(i16, s3, FT), (n16, h3, FT), (i16, h2, FT), k2]
+        mms(bk, 0, 64, qt)
+        mms(bk, 64, 128, tq)
+        vv = (B(n("vv")), ("idh", "d37", n("vv")))
+        mms(bk, 128, 192, [(i16,) + vv])
+        mms(bk, 192, 256, [(i16,) + vv])
+        mms(bk, 256, 320, qt + [(B("d37"),) + vv])
+        mms(bk, 320, 384, tq + [(B("d37"),) + vv])
+        tt(128, B(n("pp")), B(n("sr")), pb[bk][:, 0:128], A.mult, r=(n("sr"),), w=(n("pp"),), b=(bk,))
+        ts(128, B(n("qq")), B(n("pp")), 5, A.arith_shift_right, r=(n("pp"),), w=(n("qq"),))
+        tt(128, B(n("zi")), B(n("qq")), pb[bk][:, 128:256], A.mult, r=(n("qq"),), w=(n("zi"),), b=(bk,))
+        tt(128, B(n("ui")), B(n("zi")), pb[bk][:, 256:384], A.add, r=(n("zi"),), w=(n("ui"),), b=(bk,))
+        for q in range(3):
+            mms(bk, 64 * q, 64 * q + 64, [(ib, B(xr, 256, 320), ("idb", xr))])
+        ts(128, B(n("nb")), B(n("ui")), 4095, A.bitwise_and, r=(n("ui"),), w=(n("nb"),))
+        ps = n("ps")
+        ts(128, B(n("src"), 64, 192), B(n("nb")), -2048.0, A.add, r=(n("nb"),), w=(n("src") + "x",))
+        tt(64, B(ps, 0, 64), s0, pb[bk][:, 0:64], A.mult, r=(stt,), w=(ps,), b=(bk,))
+        tt(192, B(ps, 64, 256), B(n("src")), pb[bk][:, 0:192], A.mult, r=(n("src"), n("src") + "x"), w=(ps + "x",), b=(bk,))
+        SX = ("idh", "ndh", n("src"), n("src") + "x", ps, ps + "x", stt)
+        r0, a1, b1 = [B(n("src"), 64 * q, 64 * q + 64) for q in range(3)]
+        e0, er, ea, eb = [B(ps, 64 * q, 64 * q + 64) for q in range(4)]
+        pos = lambda x: (i16, x, SX)
+        neg = lambda x: (n16, x, SX)
+        mms(bk, 192, 256, [pos(a1), neg(ea), pos(e0), neg(r0), pos(er), neg(eb)])
+        mms(bk, 256, 320, [pos(a1), neg(ea), pos(e0), neg(b1), pos(eb), neg(er)])
+        gd = n("gd")
+        tt(128, B(gd), B(n("fb")), pb[bk][:, 192:320], A.mult, r=(n("fb"),), w=(gd,), b=(bk,))
+        d1, d2 = B(gd, 0, 64), B(gd, 64, 128)
+        plus = lambda x: (B("idf"), x, ("idf", gd), 4)
+        minus = lambda x: (B("ndf"), x, ("ndf", gd), 4)
+        mms(bk, 0, 64, [pos(s0), neg(e0), pos(ea)])
+        mms(bk, 64, 128, [pos(r0), neg(er), pos(eb), plus(d1)])
+        mms(bk, 128, 192, [pos(a1), neg(ea), pos(e0), minus(d1), minus(d2)])
+        mms(bk, 192, 256, [pos(b1), neg(eb), pos(er), plus(d2)])
+        snd, sdt = T["snd%d" % v], "snd%d_%d" % (v, c)
+        if v < VI - 1:
+            ts(192, snd[:, c * 192:c * 192 + 192], pb[bk][:, 64:256], 2048.0, A.add, w=(sdt,), b=(bk,))
+            nxt = "off%d" % (v + 1)
+            ts(64, T[nxt][:, c * 256:c * 256 + 64], pb[bk][:, 0:64], 2048.0, A.add, w=("%s_%d_0" % (nxt, c),), b=(bk,))
+        else:
+            act(192, snd[:, c * 192:c * 192 + 192], pb[bk][:, 64:256], F.Identity, 2048.0, w=(sdt,), b=(bk,))
+            act(64, T.ysb[:, c * 64:c * 64 + 64], pb[bk][:, 0:64], F.Identity, 2048.0, w=("off%d_%d_0" % (VI, c),), b=(bk,))
+        tr = []
+        for s in (1, 2, 3):
+            dst = T.cores[(rank + STEP[s]) % len(T.cores)]
+            rid, pid, _ = topo.addr(dst)
+            e = topo.engines(core, dst)
+            if v < VI - 1:
+                land = T["off%d" % (v + 1)][:, c * 256 + s * 64:c * 256 + s * 64 + 64]
+            else:
+                land = T.ysb[:, s * 192 + c * 64:s * 192 + c * 64 + 64]
+            tr.append(RemoteDMATransfer(dst_ids=[DstId(rid=rid, pnc=pid)], dma_engine_mask=(1 << e[2 * s - 2]) | (1 << e[2 * s - 1]),
+                                        remote_sem=T.sem["arr%d_%d" % (v, c)], src=snd[:, (c * 3 + s - 1) * 64:(c * 3 + s) * 64], dst=land))
+        op("pool", [lambda: g.remote_dma_fused(tr, local_sem=T.sem.sent)], 1000.0, (sdt,), ("go",), ext="send")
+        op(None, [], 0.0, ("go",), tuple("off%d_%d_%d" % (v + 1, c, s) for s in (1, 2, 3)), ext=("arr%d_%d" % (v, c), 6), lat=NET)
+        if c == NC - 1 and v < VI - 1:
+            cp(4, B4(), B("acc", 0, 3), r=("acc0", "acc1", "acc2"), w=("accb",))
+            mms(bk, 0, 1, [(B("wsn"), T.accb[:, q:q + 1], ("wsn", "accb")) for q in range(3)])
+            cp(1, ici[:, 3:4], pb[bk][:, 0:1], w=("i3",), b=(bk,))
+            ts(1, ici[:, 4:5], ici[:, 3:4], 31, A.bitwise_and, r=("i3",), w=("i4",))
+            w = (v + 1) % 2
+            tt(1, B("thf", w, w + 1), ici[:, 4:5], T.thi[:], A.add, r=("i4", "thi"), w=("thf%d" % w,))
+    B4 = lambda: T.accb[:, 0:3]
+
+    for v in range(VI):
+        for c in range(NC):
+            for s, h in GORDER:
+                gather(v, c, s, h)
+        for c in range(NC):
+            main(v, c)
+            crit(v, c)
+            scatter(c)
+            if v == VI - 1:
+                dma("sp", g.sync, T.yx[:, 1024 * c:1024 * c + 1024], T.xs[:, 1024 * c:1024 * c + 1024], ("dy0", "dy1", "dy3")[c], ("x%d" % c,))
+            upd(v, c)
+        if v == 0:
+            dma("sp", g.sync, T.yx[:, 3072:4096], T.xs[:, 3072:4096], "dy2", ("x3",))
+    dma("sp", g.sync, T.ys[:], T.ysb[:], "dys", tuple("off%d_%d_%d" % (VI, c, s) for c in range(NC) for s in range(4)))
+
+    if "order" not in CACHE:
+        CACHE["order"] = schedule(nodes)
+    known = {q: {} for q in Q}
+    cnt = {q: 0 for q in Q}
+    snap, ident = {}, {}
+
+    def wait(q, deps):
+        todo = sorted({d for d in deps if known[q].get(d[0], 0) < d[1]}, key=lambda d: (-len(snap.get(d, {})), d[0], -d[1]))
+        for s, k in todo:
+            if known[q].get(s, 0) >= k:
+                continue
+            Q[q].wait_ge(T.sem[s], k)
+            known[q][s] = k
+            for s2, k2 in snap.get((s, k), {}).items():
+                if known[q].get(s2, 0) < k2:
+                    known[q][s2] = k2
+    sent = 0
+    for i in CACHE["order"]:
+        x = nodes[i]
+        q = x["q"]
+        if q is None:
+            ident[i] = x["ext"]
+            continue
+        wait(q, [ident[d] for d in x["deps"] if d in ident])
+        for f in x["fns"]:
+            ins = f()
+            if x["ext"] is None:
+                cnt[q] += 1
+                ident[i] = ("s_" + q, cnt[q])
+                ins.then_inc(T.sem["s_" + q], 1)
+            elif x["ext"] == "send":
+                sent += 6
+            else:
+                ident[i] = x["ext"]
+                ins.then_inc(T.sem[x["ext"][0]], 16)
+        if i in ident:
+            snap[ident[i]] = dict(known[q])
+    known["pool"].clear()
+    wait("pool", [("s_" + q, cnt[q]) for q in ("pe", "dve", "act", "pool")] + [("sent", sent)] +
+         [(s, 16) for s in ("dx", "dh", "dt", "dy0", "dy1", "dy2", "dy3", "dys")] + [("arr%d_%d" % (v, c), 6) for v in range(VI) for c in range(NC)])

@@ -7,8 +7,12 @@ HALF = 512
 STEP = (0, 1, 2, 4)
 PAIRS = ("02", "23", "03", "13", "01", "12")
 GORDER = ((2, 0), (0, 0), (2, 1), (0, 1), (3, 0), (3, 1), (1, 0), (1, 1))
+DG = ((0, 0), (0, 1))
 
-CY, PEC, GAM, SCA, WAKE, NET = 1.0, 0.5, 1.8, 4.5, 70.0, 4000.0
+CY, PEC, GAM, SCA, WAKE, NET = 0.9, 0.45, 1.5, 3.5, 130.0, 7000.0
+TOL = 40.0
+BONUS = {'c0': 1702, 'c2': 2020, 'c1': -2022, 'u1': -2279, 'm2': -1645, 'u2': -478, 'g0': -8486, 'm1': 105, 'g1': -2946, 'm0': -4356, 'g2': -2143,
+         'u0': -1769}
 
 SCRATCH = {"xs": ("sbuf", [128, 4096], "bfloat16"), "homi": ("sbuf", [128, 768], "int32"), "lists": ("sbuf", [128, 12], "uint16"),
            "thi": ("sbuf", [128, 1], "int32"), "ysb": ("sbuf", [128, 768], "float32"), "ici": ("sbuf", [128, 8], "int32"),
@@ -35,19 +39,21 @@ def _pack(buf, dtype, names):
 
 
 for _p in range(NC):
-    for _k, _d, _l in (("h", "float16", (("ab", 128), ("c1", 64), ("y", 128), ("zz", 128), ("fs", 256), ("src", 192), ("vv", 64), ("ps", 256), ("st", 256))),
+    for _k, _d, _l in (("h", "float16", (("ab", 128), ("c1", 64), ("y", 128), ("zz", 128), ("fs", 256), ("src", 192), ("vv", 64), ("ps", 256), ("st", 256),
+                                         ("gd", 256))),
                        ("b", "bfloat16", (("u", 64), ("o", 64), ("tu", 128), ("om", 64), ("gs", 64), ("ts", 64), ("same", 64), ("xr", 320), ("fb", 128),
                                           ("tq", 64))),
-                       ("f", "float32", (("m1", 64), ("lt", 32), ("sr", 128), ("gd", 128))),
-                       ("i", "int32", (("pp", 128), ("qq", 128), ("zi", 128), ("ui", 128), ("nb", 128)))):
+                       ("f", "float32", (("m1", 64), ("lt", 32), ("sr", 128))),
+                       ("i", "int32", (("pp", 128), ("qq", 128), ("ui", 128), ("nb", 128)))):
         _pack("w%s%d" % (_k, _p), _d, [("%s_%d" % (_n, _p), _w) for _n, _w in _l])
-_pack("conh", "float16", [(_n, 128) for _n in ("idh", "ndh", "d37", "wza", "wzb", "wta", "wtb")])
+_pack("conh", "float16", [(_n, 128) for _n in ("idh", "ndh", "i4h", "d37", "wza", "wzb", "wta", "wtb")])
 _pack("conb", "bfloat16", [(_n, 128) for _n in ("idb", "onb", "wc", "ca", "cb", "wr", "wrn", "wp2", "wsn", "wl0", "wl2", "bl0", "bl2", "br0", "br2", "b2k",
                                                 "rw")] + [("red", 144), ("reds", 144), ("ale", 131), ("alo", 131), ("m192", 64)])
 _pack("conf", "float32", [("ia", 144), ("onf", 128), ("nof", 128), ("idf", 128), ("ndf", 128), ("bm", 128), ("bm0", 128), ("jj", 128), ("kc", 1), ("ek", 16),
                           ("acc", 4), ("thf", 2), ("j17", 17)] + [("t%d" % _n, 128) for _n in range(4)] + [("f%d" % _n, 17) for _n in range(8)] +
       [("q%d" % _n, 17) for _n in range(4)] + [("col%d" % _n, 1) for _n in range(40)])
 SEMAPHORES = ["s_pe", "s_dve", "s_act", "s_pool", "sent", "dx", "dh", "dt", "dy0", "dy1", "dy2", "dy3", "dys"]
+SEMAPHORES += ["ds%d_%d_%d" % (_v, _c, _j) for _v in range(VI) for _c in range(NC) for _j in range(2)]
 SEMAPHORES += ["arr%d_%d" % (_v, _c) for _v in range(VI) for _c in range(NC)]
 CACHE = {}
 
@@ -59,9 +65,11 @@ def schedule(nodes):
         for d in x["deps"] | x["odeps"]:
             succ[d].append(i)
     level = [0.0] * n
+    prio = [0.0] * n
     for i in range(n - 1, -1, -1):
         x = nodes[i]
         level[i] = x["cost"] + x["lat"] + max([level[j] + (WAKE if i in nodes[j]["deps"] else 0.0) for j in succ[i]] + [0.0])
+        prio[i] = level[i] + BONUS.get(x["lab"], 0.0)
     left = [len(x["deps"] | x["odeps"]) for x in nodes]
     ready = [0.0] * n
     free, cand, order = {}, {}, []
@@ -75,7 +83,7 @@ def schedule(nodes):
                 continue
             t = free.get(q, 0.0) if q is not None else 0.0
             first = max(t, min(ready[i] for i in l))
-            i = max((i for i in l if ready[i] <= first + 1.0), key=lambda i: (level[i], -i))
+            i = max((i for i in l if ready[i] <= first + TOL), key=lambda i: (prio[i], -i))
             if best is None or max(first, ready[i]) < best[0]:
                 best = (max(first, ready[i]), q, i)
         s, q, i = best
@@ -100,6 +108,7 @@ def rank_program(g, core, T, topo):
     Q = {"pe": g.tensor, "dve": g.vector, "act": g.scalar, "pool": g, "sp": g.sync}
     nodes, lastw, readers, banks = [], {}, {}, {}
     pb = [T["pb%d" % b] for b in range(8)]
+    lab = [None]
 
     def B(name, lo=0, hi=None, st=1):
         buf, at, w = PLACE[name]
@@ -119,7 +128,7 @@ def rank_program(g, core, T, topo):
         for t in b:
             for q2, d in banks.get(t, {}).items():
                 (odeps if q2 == q else deps).add(d)
-        nodes.append({"q": q, "fns": fns, "cost": cost, "deps": deps, "odeps": odeps - deps, "ext": ext, "lat": lat})
+        nodes.append({"q": q, "fns": fns, "cost": cost, "deps": deps, "odeps": odeps - deps, "ext": ext, "lat": lat, "lab": lab[0]})
         for t in r:
             readers.setdefault(t, set()).add(i)
         for t in w:
@@ -151,8 +160,7 @@ def rank_program(g, core, T, topo):
         def one(l, x, s, e):
             return lambda: g.tensor.matmul(out=pb[bank][:, lo:hi], lhsT=l, rhs=x, start=s, stop=e)
         fns = [one(x[0], x[1], start and j == 0, stop and j == len(terms) - 1) for j, x in enumerate(terms)]
-        cost = sum(PEC * max(64, hi - lo) * (x[3] if len(x) > 3 else 1) for x in terms)
-        op("pe", fns, cost, tuple({t for x in terms for t in x[2]}), (), (bank,))
+        op("pe", fns, PEC * max(64, hi - lo) * len(terms), tuple({t for x in terms for t in x[2]}), (), (bank,))
 
     def dma(q, eng, out, in_, sem, r=(), w=(), lat=2500.0):
         op(q, [lambda: eng.dma_start(out=out, in_=in_)], 60.0, r, w, ext=(sem, 16), lat=lat)
@@ -275,6 +283,7 @@ def rank_program(g, core, T, topo):
     k16, k16t = col(1, kc, 16.0, A.mult, r=(kct,))
     cp(128, B("idh"), B("idf"), r=("idf",), w=("idh",))
     cp(128, B("ndh"), B("ndf"), r=("ndf",), w=("ndh",))
+    ts(128, B("i4h"), B("idf"), 4096.0, A.mult, r=("idf",), w=("i4h",))
     k37, k37t = col(1, kc, 37.0, A.mult, r=(kct,))
     ts(128, B("d37"), B("idf"), k37, A.mult, r=("idf", k37t), w=("d37",))
     both("wr", B("wr"), 128, B("jj"), kc, A.is_ge, B("bm"), 1.0, A.mult, A.mult, ("jj", kct, "bm"))
@@ -296,12 +305,16 @@ def rank_program(g, core, T, topo):
     def gather(v, c, s, h):
         lo = c * 256 + s * 64 + h * 32
         at = c * 1024 + h * HALF
-        act(0, T["g%d" % s][:, at:at + HALF], T.xs[:, 0:4096].indirect(T["off%d" % v][:, lo:lo + 32]), F.Copy,
-            r=("x0", "x1", "x2", "x3", "off%d_%d_%d" % (v, c, s)), w=("g%d_%d_%d" % (s, c, h),), cost=70 + GAM * HALF)
+        out, in_ = T["g%d" % s][:, at:at + HALF], T.xs[:, 0:4096].indirect(T["off%d" % v][:, lo:lo + 32])
+        r, w = ("x0", "x1", "x2", "x3", "off%d_%d_%d" % (v, c, s)), ("g%d_%d_%d" % (s, c, h),)
+        if c == 0 and (s, h) in DG:
+            cp(0, out, in_, r=r, w=w, cost=60 + GAM * HALF)
+        else:
+            act(0, out, in_, F.Copy, r=r, w=w, cost=70 + GAM * HALF)
     uc = [0]
 
     def ufill(c, s, h):
-        bank = uc[0] % 4
+        bank = uc[0] % 3
         uc[0] += 1
         at = c * 1024 + h * HALF
         mms(bank, 0, 512, [(B("idb"), T["g%d" % s][:, at:at + HALF], ("idb", "g%d_%d_%d" % (s, c, h)))])
@@ -319,41 +332,49 @@ def rank_program(g, core, T, topo):
             mms(bank, at, at + 64, [(B("red", 15 - k, 143 - k), d[:, k:1024:16], toks) for k in range(8 * q, 8 * q + 8)],
                 first and q == 0, last and q == 1)
 
-    def total(c):
-        for q, s in enumerate((2, 0, 3, 1)):
+    def add_up(v, c):
+        for j, (to_, s) in enumerate(((3, 2), (1, 0))):
+            toks = ["g%d_%d_%d" % (z, c, h) for z in (s, to_) for h in range(2)]
+            out, in_ = T["g%d" % to_][:, c * 1024:c * 1024 + 1024], T["g%d" % s][:, c * 1024:c * 1024 + 1024]
+            op("pool", [(lambda o_, i_: lambda: g.dma_start(out=o_, in_=i_, accum_op=A.add))(out, in_)], 1000.0, toks, toks[2:],
+               ext=("ds%d_%d_%d" % (v, c, j), 16), lat=3500.0)
+
+    def total(c, bk):
+        for q, s in enumerate((3, 1)):
             for e in range(2):
-                mms(5, 64, 128, [(B("reds", 15 - k, 143 - k), T["g%d" % s][:, c * 1024 + k:c * 1024 + 1024:16],
-                                  ("reds", "g%d_%d_0" % (s, c), "g%d_%d_1" % (s, c))) for k in range(8 * e, 8 * e + 8)], q == 0 and e == 0, q == 3 and e == 1)
+                mms(bk, 384, 448, [(B("reds", 15 - k, 143 - k), T["g%d" % s][:, c * 1024 + k:c * 1024 + 1024:16],
+                                    ("reds", "g%d_%d_0" % (s, c), "g%d_%d_1" % (s, c))) for k in range(8 * e, 8 * e + 8)], q + e == 0, q + e == 2)
 
     def main(v, c):
         par = (v * NC + c) % 2
         u2 = [ufill(c, 2, 0), ufill(c, 2, 1)]
         pair(c, par, 0, u2[0], "02", 0)
         pair(c, par, 0, u2[1], "02", 1)
-        u3 = [ufill(c, 3, 0), ufill(c, 3, 1)]
         red(par, "02", 4, 0, True, False)
         pair(c, par, 3, u2[0], "23", 0)
         pair(c, par, 3, u2[1], "23", 1)
-        u1 = [ufill(c, 1, 0), ufill(c, 1, 1)]
         red(par, "23", 5, 0, True, False)
+        u3 = [ufill(c, 3, 0)]
         pair(c, par, 0, u3[0], "03", 0)
+        u3.append(ufill(c, 3, 1))
         pair(c, par, 0, u3[1], "03", 1)
         pair(c, par, 1, u3[0], "13", 0)
         pair(c, par, 1, u3[1], "13", 1)
         red(par, "13", 4, 0, False, True)
+        u1 = [ufill(c, 1, 0)]
         pair(c, par, 0, u1[0], "01", 0)
+        u1.append(ufill(c, 1, 1))
         pair(c, par, 0, u1[1], "01", 1)
         red(par, "01", 5, 0, False, True)
         m1 = "m1_%d" % c
-        cp(64, B(m1), pb[4][:, 0:64], w=(m1,), b=(4,))
+        act(64, B(m1), pb[4][:, 0:64], F.Copy, w=(m1,), b=(4,))
         red(par, "03", 4, 64, True, False)
         tt(64, B("ab_%d" % c, 0, 64), pb[5][:, 0:64], B(m1), A.subtract, r=(m1,), w=("a_%d" % c,), b=(5,))
         pair(c, par, 2, u1[0], "12", 0)
         pair(c, par, 2, u1[1], "12", 1)
         red(par, "12", 4, 64, False, True)
         tt(64, B("ab_%d" % c, 64, 128), pb[4][:, 64:128], B(m1), A.subtract, r=(m1,), w=("b_%d" % c,), b=(4,))
-        total(c)
-        tt(64, B("c1_%d" % c), B(m1), pb[5][:, 64:128], A.subtract, r=(m1,), w=("c1_%d" % c,), b=(5,))
+        add_up(v, c)
 
     def crit(v, c):
         bk = 6
@@ -377,7 +398,11 @@ def rank_program(g, core, T, topo):
         op("dve", [lambda: g.vector.transpose(out=B(n("lt")), in_=pb[bk][:, 448:480])], 64, (), (n("lt"),), (bk,))
         li, lit = T.lists[:, 4 * c:4 * c + 4], n("li")
         ts(4, li, B(n("lt"), 0, 4), k16, A.add, r=(n("lt"), k16t), w=(lit,))
-        cp(64, B(n("gs")), T.g0[:, c * 1024:c * 1024 + 1024].indirect(li), r=(lit, "g0_%d_0" % c, "g0_%d_1" % c), w=(n("gs"),), cost=60 + 64 * GAM)
+        gr = (lit, "g0_%d_0" % c, "g0_%d_1" % c)
+        if c < NC - 1:
+            act(64, B(n("gs")), T.g0[:, c * 1024:c * 1024 + 1024].indirect(li), F.Copy, r=gr, w=(n("gs"),), cost=75 + 64 * GAM)
+        else:
+            cp(64, B(n("gs")), T.g0[:, c * 1024:c * 1024 + 1024].indirect(li), r=gr, w=(n("gs"),), cost=60 + 64 * GAM)
         tt(64, B(n("ts")), T.xs[:, c * 1024:c * 1024 + 1024].indirect(li), B(n("gs")), A.add, r=(lit, n("gs"), "x%d" % c), w=(n("ts"),), cost=60 + 64 * GAM)
         ts(64, B(n("tq")), B(n("ts")), 0.5, A.mult, 191.75, A.add, r=(n("ts"),), w=(n("tq"),))
 
@@ -386,13 +411,13 @@ def rank_program(g, core, T, topo):
            r=("tq_%d" % c, "m192", "li_%d" % c), w=("x%d" % c,), cost=60 + 64 * SCA)
 
     def upd(v, c):
-        bk = 7
+        bk, bz = 7, 3
         n = lambda s: "%s_%d" % (s, c)
         st, stt = B(n("st")), n("st")
         i16, n16, ib = B("idh"), B("ndh"), B("idb")
         ts(256, st, T["off%d" % v][:, c * 256:c * 256 + 256], -2048.0, A.add, r=tuple("off%d_%d_%d" % (v, c, s) for s in range(4)), w=(stt,))
-        mms(bk, 448, 512, [(B("wp2"), B(n("o")), ("wp2", n("o")))])
-        act(64, B(n("same")), pb[bk][:, 448:512], F.Relu, -1.0, accum=B("acc", c, c + 1), w=(n("same"), "acc%d" % c), b=(bk,))
+        mms(bz, 448, 512, [(B("wp2"), B(n("o")), ("wp2", n("o")))])
+        act(64, B(n("same")), pb[bz][:, 448:512], F.Relu, -1.0, accum=B("acc", c, c + 1), w=(n("same"), "acc%d" % c), b=(bz,))
         o, om = B(n("o")), B(n("om"))
         for q, (m, w) in enumerate((("bl0", "wrn"), ("br0", "wr"), ("bl2", "wrn"), ("br2", "wr"))):
             mms(bk, 64 * q, 64 * q + 64, [(B(m), o, (m, n("o"))), (B(w), om, (w, n("om")))])
@@ -401,20 +426,20 @@ def rank_program(g, core, T, topo):
         act(320, B(xr), pb[bk][:, 0:320], F.Relu, w=(xr,), b=(bk,))
         for q in range(4):
             a = q // 2 * 128
-            mms(bk, 64 * q, 64 * q + 64, [(ib, B(xr, a, a + 64), ("idb", xr)), (ib, B(xr, a + 64, a + 128), ("idb", xr))])
+            mms(bz, 64 * q, 64 * q + 64, [(ib, B(xr, a, a + 64), ("idb", xr)), (ib, B(xr, a + 64, a + 128), ("idb", xr))])
         fs = n("fs")
-        tt(128, B(fs, 0, 128), B(stt, 64, 192), pb[bk][:, 0:128], A.mult, r=(stt,), w=(fs,), b=(bk,))
-        tt(128, B(fs, 128, 256), B(stt, 128, 256), pb[bk][:, 128:256], A.mult, r=(stt,), w=(fs + "x",), b=(bk,))
-        tt(128, B(n("zz")), B(n("ab")), pb[bk][:, 64:192], A.mult, r=(n("a"), n("b")), w=(n("zz"),), b=(bk,))
-        act(128, B(n("fb")), pb[bk][:, 64:192], F.Copy, w=(n("fb"),), b=(bk,))
+        total(c, 5)
+        tt(64, B(n("c1")), B(n("m1")), pb[5][:, 384:448], A.subtract, r=(n("m1"),), w=(n("c1"),), b=(5,))
+        tt(128, B(fs, 0, 128), B(stt, 64, 192), pb[bz][:, 0:128], A.mult, r=(stt,), w=(fs,), b=(bz,))
+        tt(128, B(fs, 128, 256), B(stt, 128, 256), pb[bz][:, 128:256], A.mult, r=(stt,), w=(fs + "x",), b=(bz,))
+        tt(128, B(n("zz")), B(n("ab")), pb[bz][:, 64:192], A.mult, r=(n("a"), n("b")), w=(n("zz"),), b=(bz,))
+        act(128, B(n("fb")), pb[bz][:, 64:192], F.Copy, w=(n("fb"),), b=(bz,))
+        mms(5, 384, 448, [(i16, B(n("c1")), ("idh", n("c1"))), (i16, B(n("zz"), 0, 64), ("idh", n("zz"))), (i16, B(n("zz"), 64, 128), ("idh", n("zz")))])
+        ts(64, B(n("vv")), pb[5][:, 384:448], B("thf", v % 2, v % 2 + 1), A.is_gt, r=("thf%d" % (v % 2),), w=(n("vv"),), b=(5,))
         f1, f2, h2, h3 = B(fs, 0, 64), B(fs, 64, 128), B(fs, 128, 192), B(fs, 192, 256)
         s0, s1, s2, s3 = [B(stt, 64 * q, 64 * q + 64) for q in range(4)]
         FT = ("idh", "ndh", stt, fs, fs + "x")
-        mms(bk, 256, 320, [(i16, s0, FT)])
         mms(bk, 320, 384, [(i16, s1, FT), (n16, f1, FT), (i16, f2, FT)])
-        mms(bk, 384, 448, [(i16, B(n("c1")), ("idh", n("c1"))), (i16, B(n("zz"), 0, 64), ("idh", n("zz"))), (i16, B(n("zz"), 64, 128), ("idh", n("zz")))])
-        act(128, B(n("sr")), pb[bk][:, 256:384], F.Identity, 2048.0, w=(n("sr"),), b=(bk,))
-        ts(64, B(n("vv")), pb[bk][:, 384:448], B("thf", v % 2, v % 2 + 1), A.is_gt, r=("thf%d" % (v % 2),), w=(n("vv"),), b=(bk,))
         cp(64, B(n("src"), 0, 64), pb[bk][:, 320:384], w=(n("src"),), b=(bk,))
         k2 = (B("b2k"), o, ("b2k", n("o")))
         qt = [(i16, s2, FT), (i16, f1, FT), (n16, f2, FT), (i16, h3, FT), (n16, h2, FT), k2]
@@ -422,14 +447,15 @@ def rank_program(g, core, T, topo):
         mms(bk, 0, 64, qt)
         mms(bk, 64, 128, tq)
         vv = (B(n("vv")), ("idh", "d37", n("vv")))
-        mms(bk, 128, 192, [(i16,) + vv])
-        mms(bk, 192, 256, [(i16,) + vv])
-        mms(bk, 256, 320, qt + [(B("d37"),) + vv])
-        mms(bk, 320, 384, tq + [(B("d37"),) + vv])
+        v4 = (B("i4h"), B(n("vv")), ("i4h", n("vv")))
+        mms(bz, 128, 192, [(i16, s0, FT), v4])
+        mms(bz, 192, 256, [(i16, B(n("src"), 0, 64), ("idh", n("src"))), v4])
+        act(128, B(n("sr")), pb[bz][:, 128:256], F.Relu, b=(bz,), bias=-2048.0, w=(n("sr"),))
+        mms(bz, 256, 320, qt + [(B("d37"),) + vv])
+        mms(bz, 320, 384, tq + [(B("d37"),) + vv])
         tt(128, B(n("pp")), B(n("sr")), pb[bk][:, 0:128], A.mult, r=(n("sr"),), w=(n("pp"),), b=(bk,))
         ts(128, B(n("qq")), B(n("pp")), 5, A.arith_shift_right, r=(n("pp"),), w=(n("qq"),))
-        tt(128, B(n("zi")), B(n("qq")), pb[bk][:, 128:256], A.mult, r=(n("qq"),), w=(n("zi"),), b=(bk,))
-        tt(128, B(n("ui")), B(n("zi")), pb[bk][:, 256:384], A.add, r=(n("zi"),), w=(n("ui"),), b=(bk,))
+        tt(128, B(n("ui")), B(n("qq")), pb[bz][:, 256:384], A.add, r=(n("qq"),), w=(n("ui"),), b=(bz,))
         for q in range(3):
             mms(bk, 64 * q, 64 * q + 64, [(ib, B(xr, 256, 320), ("idb", xr))])
         ts(128, B(n("nb")), B(n("ui")), 4095, A.bitwise_and, r=(n("ui"),), w=(n("nb"),))
@@ -437,22 +463,25 @@ def rank_program(g, core, T, topo):
         ts(128, B(n("src"), 64, 192), B(n("nb")), -2048.0, A.add, r=(n("nb"),), w=(n("src") + "x",))
         tt(64, B(ps, 0, 64), s0, pb[bk][:, 0:64], A.mult, r=(stt,), w=(ps,), b=(bk,))
         tt(192, B(ps, 64, 256), B(n("src")), pb[bk][:, 0:192], A.mult, r=(n("src"), n("src") + "x"), w=(ps + "x",), b=(bk,))
-        SX = ("idh", "ndh", n("src"), n("src") + "x", ps, ps + "x", stt)
         r0, a1, b1 = [B(n("src"), 64 * q, 64 * q + 64) for q in range(3)]
         e0, er, ea, eb = [B(ps, 64 * q, 64 * q + 64) for q in range(4)]
-        pos = lambda x: (i16, x, SX)
-        neg = lambda x: (n16, x, SX)
-        mms(bk, 192, 256, [pos(a1), neg(ea), pos(e0), neg(r0), pos(er), neg(eb)])
-        mms(bk, 256, 320, [pos(a1), neg(ea), pos(e0), neg(b1), pos(eb), neg(er)])
         gd = n("gd")
-        tt(128, B(gd), B(n("fb")), pb[bk][:, 192:320], A.mult, r=(n("fb"),), w=(gd,), b=(bk,))
-        d1, d2 = B(gd, 0, 64), B(gd, 64, 128)
-        plus = lambda x: (B("idf"), x, ("idf", gd), 4)
-        minus = lambda x: (B("ndf"), x, ("ndf", gd), 4)
+        SX = ["idh", "ndh", n("src"), n("src") + "x", ps, ps + "x", stt]
+        pos = lambda x: (i16, x, tuple(SX))
+        neg = lambda x: (n16, x, tuple(SX))
+        nq, nr, nt = [pos(a1), neg(ea), pos(e0)], [pos(r0), neg(er), pos(eb)], [pos(b1), neg(eb), pos(er)]
+        mms(bz, 192, 256, nq)
+        mms(bz, 256, 320, nr)
+        mms(bz, 320, 384, nt)
+        tt(64, B(gd, 0, 64), B(n("fb"), 0, 64), pb[bz][:, 192:256], A.mult, r=(n("fb"),), w=(gd,), b=(bz,))
+        tt(64, B(gd, 64, 128), B(n("fb"), 64, 128), pb[bz][:, 192:256], A.mult, r=(n("fb"),), w=(gd + "x",), b=(bz,))
+        tt(128, B(gd, 128, 256), B(n("fb")), pb[bz][:, 256:384], A.mult, r=(n("fb"),), w=(gd + "y",), b=(bz,))
+        SX += [gd, gd + "x", gd + "y"]
+        q1, q3, p1, p3 = [B(gd, 64 * q, 64 * q + 64) for q in range(4)]
         mms(bk, 0, 64, [pos(s0), neg(e0), pos(ea)])
-        mms(bk, 64, 128, [pos(r0), neg(er), pos(eb), plus(d1)])
-        mms(bk, 128, 192, [pos(a1), neg(ea), pos(e0), minus(d1), minus(d2)])
-        mms(bk, 192, 256, [pos(b1), neg(eb), pos(er), plus(d2)])
+        mms(bk, 64, 128, nr + [neg(p1), pos(q1)])
+        mms(bk, 128, 192, nq + [neg(q1), pos(p1), neg(q3), pos(p3)])
+        mms(bk, 192, 256, nt + [neg(p3), pos(q3)])
         snd, sdt = T["snd%d" % v], "snd%d_%d" % (v, c)
         if v < VI - 1:
             ts(192, snd[:, c * 192:c * 192 + 192], pb[bk][:, 64:256], 2048.0, A.add, w=(sdt,), b=(bk,))
@@ -475,22 +504,25 @@ def rank_program(g, core, T, topo):
         op("pool", [lambda: g.remote_dma_fused(tr, local_sem=T.sem.sent)], 1000.0, (sdt,), ("go",), ext="send")
         op(None, [], 0.0, ("go",), tuple("off%d_%d_%d" % (v + 1, c, s) for s in (1, 2, 3)), ext=("arr%d_%d" % (v, c), 6), lat=NET)
         if c == NC - 1 and v < VI - 1:
-            cp(4, B4(), B("acc", 0, 3), r=("acc0", "acc1", "acc2"), w=("accb",))
+            cp(4, T.accb[:, 0:3], B("acc", 0, 3), r=("acc0", "acc1", "acc2"), w=("accb",))
             mms(bk, 0, 1, [(B("wsn"), T.accb[:, q:q + 1], ("wsn", "accb")) for q in range(3)])
             cp(1, ici[:, 3:4], pb[bk][:, 0:1], w=("i3",), b=(bk,))
             ts(1, ici[:, 4:5], ici[:, 3:4], 31, A.bitwise_and, r=("i3",), w=("i4",))
             w = (v + 1) % 2
             tt(1, B("thf", w, w + 1), ici[:, 4:5], T.thi[:], A.add, r=("i4", "thi"), w=("thf%d" % w,))
-    B4 = lambda: T.accb[:, 0:3]
 
     for v in range(VI):
         for c in range(NC):
+            lab[0] = "g%d" % c
             for s, h in GORDER:
                 gather(v, c, s, h)
         for c in range(NC):
+            lab[0] = "m%d" % c
             main(v, c)
+            lab[0] = "c%d" % c
             crit(v, c)
             scatter(c)
+            lab[0] = "u%d" % c
             if v == VI - 1:
                 dma("sp", g.sync, T.yx[:, 1024 * c:1024 * c + 1024], T.xs[:, 1024 * c:1024 * c + 1024], ("dy0", "dy1", "dy3")[c], ("x%d" % c,))
             upd(v, c)
@@ -502,7 +534,7 @@ def rank_program(g, core, T, topo):
         CACHE["order"] = schedule(nodes)
     known = {q: {} for q in Q}
     cnt = {q: 0 for q in Q}
-    snap, ident = {}, {}
+    snap, ident, seen = {}, {}, set()
 
     def wait(q, deps):
         todo = sorted({d for d in deps if known[q].get(d[0], 0) < d[1]}, key=lambda d: (-len(snap.get(d, {})), d[0], -d[1]))
@@ -510,6 +542,7 @@ def rank_program(g, core, T, topo):
             if known[q].get(s, 0) >= k:
                 continue
             Q[q].wait_ge(T.sem[s], k)
+            seen.add((s, k))
             known[q][s] = k
             for s2, k2 in snap.get((s, k), {}).items():
                 if known[q].get(s2, 0) < k2:
@@ -535,6 +568,8 @@ def rank_program(g, core, T, topo):
                 ins.then_inc(T.sem[x["ext"][0]], 16)
         if i in ident:
             snap[ident[i]] = dict(known[q])
+    ends = [("s_" + q, cnt[q]) for q in ("pe", "dve", "act", "pool")] + [("sent", sent)]
+    ends += [(s, 6 if s[:3] == "arr" else 16) for s in SEMAPHORES if s[:2] != "s_" and s != "sent"]
     known["pool"].clear()
-    wait("pool", [("s_" + q, cnt[q]) for q in ("pe", "dve", "act", "pool")] + [("sent", sent)] +
-         [(s, 16) for s in ("dx", "dh", "dt", "dy0", "dy1", "dy2", "dy3", "dys")] + [("arr%d_%d" % (v, c), 6) for v in range(VI) for c in range(NC)])
+    snap.clear()
+    wait("pool", [e for e in ends if e not in seen])

from concourse.bass import DstId, RemoteDMATransfer
from concourse.mybir import AluOpType as A, ActivationFunctionType as F

VI = 4
NC = 3
HALF = 512
STEP = (0, 1, 2, 4)
PAIRS = ("02", "23", "03", "13", "01", "12")
GORDER = ((2, 0), (0, 0), (2, 1), (0, 1), (3, 0), (3, 1), (1, 0), (1, 1))
DG = ((0, 0), (0, 1))

CY, PEC, GAM, SCA, WAKE, NET = 0.9, 0.45, 1.5, 3.5, 130.0, 7000.0
TOL = 40.0
BONUS = {'c0': 1702, 'c2': 2020, 'c1': -2022, 'u1': -2279, 'm2': -1645, 'u2': -478, 'g0': -8486, 'm1': 105, 'g1': -2946, 'm0': -4356, 'g2': -2143,
         'u0': -1769}

SCRATCH = {"xs": ("sbuf", [128, 4096], "bfloat16"), "homi": ("sbuf", [128, 768], "int32"), "lists": ("sbuf", [128, 12], "uint16"),
           "thi": ("sbuf", [128, 1], "int32"), "ysb": ("sbuf", [128, 768], "float32"), "ici": ("sbuf", [128, 8], "int32"),
           "ip": ("sbuf", [128, 1], "int32"), "accb": ("sbuf", [128, 4], "bfloat16")}
PLACE = {}
for _v in range(VI):
    SCRATCH["off%d" % _v] = ("sbuf", [128, 768], "uint16")
    SCRATCH["snd%d" % _v] = ("sbuf", [128, 576], "uint16" if _v < VI - 1 else "float32")
for _s in range(4):
    SCRATCH["g%d" % _s] = ("sbuf", [128, 3072], "bfloat16")
for _b in range(8):
    SCRATCH["pb%d" % _b] = ("psum", [128, 512], "float32")
for _p in range(2):
    for _n in PAIRS:
        SCRATCH["d%s_%d" % (_n, _p)] = ("sbuf", [128, 1024], "bfloat16")


def _pack(buf, dtype, names):
    at = 0
    for n, w in names:
        PLACE[n] = (buf, at, w)
        at += (w + 15) // 16 * 16
    SCRATCH[buf] = ("sbuf", [128, at], dtype)


for _p in range(NC):
    for _k, _d, _l in (("h", "float16", (("ab", 128), ("c1", 64), ("y", 128), ("zz", 128), ("fs", 256), ("src", 192), ("vv", 64), ("ps", 256), ("st", 256),
                                         ("gd", 256))),
                       ("b", "bfloat16", (("u", 64), ("o", 64), ("tu", 128), ("om", 64), ("gs", 64), ("ts", 64), ("same", 64), ("xr", 320), ("fb", 128),
                                          ("tq", 64))),
                       ("f", "float32", (("m1", 64), ("lt", 32), ("sr", 128))),
                       ("i", "int32", (("pp", 128), ("qq", 128), ("ui", 128), ("nb", 128)))):
        _pack("w%s%d" % (_k, _p), _d, [("%s_%d" % (_n, _p), _w) for _n, _w in _l])
_pack("conh", "float16", [(_n, 128) for _n in ("idh", "ndh", "i4h", "d37", "wza", "wzb", "wta", "wtb")])
_pack("conb", "bfloat16", [(_n, 128) for _n in ("idb", "onb", "wc", "ca", "cb", "wr", "wrn", "wp2", "wsn", "wl0", "wl2", "bl0", "bl2", "br0", "br2", "b2k",
                                                "rw")] + [("red", 144), ("reds", 144), ("ale", 131), ("alo", 131), ("m192", 64)])
_pack("conf", "float32", [("ia", 144), ("onf", 128), ("nof", 128), ("idf", 128), ("ndf", 128), ("bm", 128), ("bm0", 128), ("jj", 128), ("kc", 1), ("ek", 16),
                          ("acc", 4), ("thf", 2), ("j17", 17)] + [("t%d" % _n, 128) for _n in range(4)] + [("f%d" % _n, 17) for _n in range(8)] +
      [("q%d" % _n, 17) for _n in range(4)] + [("col%d" % _n, 1) for _n in range(40)])
SEMAPHORES = ["s_pe", "s_dve", "s_act", "s_pool", "sent", "dx", "dh", "dt", "dy0", "dy1", "dy2", "dy3", "dys"]
SEMAPHORES += ["ds%d_%d_%d" % (_v, _c, _j) for _v in range(VI) for _c in range(NC) for _j in range(2)]
SEMAPHORES += ["arr%d_%d" % (_v, _c) for _v in range(VI) for _c in range(NC)]
CACHE = {}


def schedule(nodes):
    n = len(nodes)
    succ = [[] for _ in range(n)]
    for i, x in enumerate(nodes):
        for d in x["deps"] | x["odeps"]:
            succ[d].append(i)
    level = [0.0] * n
    prio = [0.0] * n
    for i in range(n - 1, -1, -1):
        x = nodes[i]
        level[i] = x["cost"] + x["lat"] + max([level[j] + (WAKE if i in nodes[j]["deps"] else 0.0) for j in succ[i]] + [0.0])
        prio[i] = level[i] + BONUS.get(x["lab"], 0.0)
    left = [len(x["deps"] | x["odeps"]) for x in nodes]
    ready = [0.0] * n
    free, cand, order = {}, {}, []
    for i, x in enumerate(nodes):
        if left[i] == 0:
            cand.setdefault(x["q"], []).append(i)
    while len(order) < n:
        best = None
        for q, l in cand.items():
            if not l:
                continue
            t = free.get(q, 0.0) if q is not None else 0.0
            first = max(t, min(ready[i] for i in l))
            i = max((i for i in l if ready[i] <= first + TOL), key=lambda i: (prio[i], -i))
            if best is None or max(first, ready[i]) < best[0]:
                best = (max(first, ready[i]), q, i)
        s, q, i = best
        cand[q].remove(i)
        order.append(i)
        x = nodes[i]
        free[q] = s + x["cost"]
        end = s + x["cost"] + x["lat"]
        for j in succ[i]:
            e = end + WAKE if i in nodes[j]["deps"] else s + x["cost"]
            ready[j] = max(ready[j], e)
            left[j] -= 1
            if left[j] == 0:
                cand.setdefault(nodes[j]["q"], []).append(j)
    return order


def rank_program(g, core, T, topo):
    rank = T.rank_of(core)
    if rank is None:
        return
    Q = {"pe": g.tensor, "dve": g.vector, "act": g.scalar, "pool": g, "sp": g.sync}
    nodes, lastw, readers, banks = [], {}, {}, {}
    pb = [T["pb%d" % b] for b in range(8)]
    lab = [None]

    def B(name, lo=0, hi=None, st=1):
        buf, at, w = PLACE[name]
        hi = w if hi is None else hi
        return T[buf][:, at + lo:at + hi:st] if st > 1 else T[buf][:, at + lo:at + hi]

    def op(q, fns, cost, r=(), w=(), b=(), ext=None, lat=0.0):
        i = len(nodes)
        deps, odeps = set(), set()
        for t in r:
            if t in lastw:
                deps.add(lastw[t])
        for t in w:
            if t in lastw:
                deps.add(lastw[t])
            deps |= readers.get(t, set())
        for t in b:
            for q2, d in banks.get(t, {}).items():
                (odeps if q2 == q else deps).add(d)
        nodes.append({"q": q, "fns": fns, "cost": cost, "deps": deps, "odeps": odeps - deps, "ext": ext, "lat": lat, "lab": lab[0]})
        for t in r:
            readers.setdefault(t, set()).add(i)
        for t in w:
            lastw[t] = i
            readers[t] = set()
        for t in b:
            banks.setdefault(t, {})[q] = i
        return i

    def tt(n, out, in0, in1, o, r=(), w=(), b=(), cost=None):
        op("dve", [lambda: g.vector.tensor_tensor(out=out, in0=in0, in1=in1, op=o)], cost or CY * max(64, n * (1 if b else 2)), r, w, b)

    def ts(n, out, in0, s1, o0, s2=None, o1=None, r=(), w=(), b=()):
        if o1 is None:
            op("dve", [lambda: g.vector.tensor_scalar(out=out, in0=in0, scalar1=s1, scalar2=None, op0=o0)], CY * max(64, n), r, w, b)
        else:
            op("dve", [lambda: g.vector.tensor_scalar(out=out, in0=in0, scalar1=s1, scalar2=s2, op0=o0, op1=o1)], CY * max(64, n), r, w, b)

    def cp(n, out, in_, r=(), w=(), b=(), cost=None):
        op("dve", [lambda: g.vector.tensor_copy(out=out, in_=in_)], cost or CY * max(64, n), r, w, b)

    def act(n, out, in_, func, bias=0.0, accum=None, r=(), w=(), b=(), cost=None):
        if accum is None:
            op("act", [lambda: g.scalar.activation(out=out, in_=in_, func=func, bias=bias)], cost or CY * max(64, n), r, w, b)
        else:
            op("act", [lambda: g.scalar.activation(out=out, in_=in_, func=func, bias=bias, accum_out=accum)], cost or CY * max(64, n), r, w, b)

    def mms(bank, lo, hi, terms, start=True, stop=True):
        def one(l, x, s, e):
            return lambda: g.tensor.matmul(out=pb[bank][:, lo:hi], lhsT=l, rhs=x, start=s, stop=e)
        fns = [one(x[0], x[1], start and j == 0, stop and j == len(terms) - 1) for j, x in enumerate(terms)]
        op("pe", fns, PEC * max(64, hi - lo) * len(terms), tuple({t for x in terms for t in x[2]}), (), (bank,))

    def dma(q, eng, out, in_, sem, r=(), w=(), lat=2500.0):
        op(q, [lambda: eng.dma_start(out=out, in_=in_)], 60.0, r, w, ext=(sem, 16), lat=lat)

    dma("sp", g.sync, T.homi[:], T.hom[:], "dh", (), ("homi",), 3500.0)
    dma("sp", g.sync, T.xs[:], T.x[:], "dx", (), ("x0", "x1", "x2", "x3"), 6500.0)
    dma("act", g.scalar, T.thi[:], T.th[:], "dt", (), ("thi",))

    def iota(out, pattern, base, cm, w, n, flag=True):
        if flag:
            op("pool", [lambda: g.iota(out, pattern, base, cm, allow_small_or_imprecise_dtypes=True)], 160 + 2 * n, (), (w,))
        else:
            op("pool", [lambda: g.iota(out, pattern, base, cm)], 160 + 2 * n, (), (w,))

    def sel(out, in_, pattern, o, base, cm, r, w):
        op("pool", [lambda: g.affine_select(out, in_, pattern, o, 0.0, base, cm)], 480, r, (w,))

    def fill(name, x):
        op("dve", [lambda: g.vector.memset(B(name), x)], 128, (), (name,))
    iota(T.ip[:], [[0, 1]], 0, 1, "ip", 1, False)
    iota(B("ia"), [[1, 144]], 0, 0, "ia", 144)
    fill("onb", 1.0)
    fill("onf", 1.0)
    fill("nof", -1.0)
    fill("m192", -192.0)
    EYE = [[-1, 128]]
    sel(B("idb"), B("onb"), EYE, A.is_equal, 0, 1, ("onb",), "idb")
    iota(B("jj"), [[0, 8], [1, 16]], 0, 0, "jj", 128)
    sel(B("bm0"), B("onf"), [[-16, 8], [0, 16]], A.is_ge, 0, 1, ("onf",), "bm0")
    sel(B("bm"), B("bm0"), [[16, 8], [0, 16]], A.is_ge, 15, -1, ("bm0",), "bm")
    sel(B("idf"), B("onf"), EYE, A.is_equal, 0, 1, ("onf",), "idf")
    sel(B("ndf"), B("nof"), EYE, A.is_equal, 0, 1, ("nof",), "ndf")
    iota(B("rw"), [[0, 4], [256, 32]], 0, 0, "rw", 128)
    ncol = [0]

    def col(n, in_, s1, o0, s2=None, o1=None, r=()):
        name = "col%d" % ncol[0]
        ncol[0] += 1
        ts(n, B(name), in_, s1, o0, s2, o1, r=r, w=(name,))
        return B(name), name
    ici = T.ici
    ts(1, ici[:, 0:1], T.ip[:], 15, A.bitwise_and, r=("ip",), w=("i0",))
    ts(1, ici[:, 1:2], T.ip[:], 31, A.bitwise_and, r=("ip",), w=("i1",))
    ts(1, ici[:, 2:3], T.ip[:], 16, A.bitwise_and, r=("ip",), w=("i2",))
    pc, pct = col(1, T.ip[:], 0.0, A.add, r=("ip",))
    kc, kct = B("kc"), "kc"
    cp(1, kc, ici[:, 0:1], r=("i0",), w=(kct,))
    tgb, tgbt = col(1, kc, -1.0, A.mult, pc, A.add, r=(kct, pct))
    tgc, tgct = col(1, tgb, 15.0, A.add, r=(tgbt,))
    ts(144, B("red"), B("ia"), tgc, A.is_equal, 2.0, A.mult, r=("ia", tgct), w=("red",))
    ts(144, B("reds"), B("ia"), tgc, A.is_equal, r=("ia", tgct), w=("reds",))
    ts(128, B("t0"), B("bm"), -512.0, A.mult, 512.0, A.add, r=("bm",), w=("t0",))
    tt(128, B("jj"), B("jj"), B("t0"), A.add, r=("jj", "t0"), w=("jj",))
    ts(16, B("ek"), B("ia", 0, 16), kc, A.is_equal, r=("ia", kct), w=("ek",))
    cp(16, B("j17", 0, 16), B("ia", 0, 16), r=("ia",), w=("j17",))
    cp(1, B("j17", 16, 17), kc, r=(kct,), w=("j17k",))
    JT = ("j17", "j17k")

    def fn(dst, start, steps):
        for q, (co, t) in enumerate(steps):
            tmp = "q%d" % (q % 4)
            ts(17, B(tmp), B("j17"), float(t), A.is_ge, float(co), A.mult, r=JT, w=(tmp,))
            if q == 0 and start is None:
                tt(17, B(dst), B("j17"), B(tmp), A.add, r=JT + (tmp,), w=(dst,))
            elif q == 0:
                ts(17, B(dst), B(tmp), float(start), A.add, r=(tmp,), w=(dst,))
            else:
                tt(17, B(dst), B(dst), B(tmp), A.add, r=(tmp, dst), w=(dst,))

    def both(name, out, n, in0, s1, o1, in1, s2, o2, mix, r):
        ts(n, B("t0", 0, n), in0, s1, o1, r=r, w=("t0",))
        ts(n, B("t1", 0, n), in1, s2, o2, r=r, w=("t1",))
        tt(n, out, B("t0", 0, n), B("t1", 0, n), mix, r=("t0", "t1"), w=(name,))

    def signs(name, p, m):
        both(name, B(name), 128, B("jj"), B(p, 16, 17), A.is_equal, B("jj"), B(m, 16, 17), A.is_equal, A.subtract, ("jj", p, m))

    def window(name, p, m):
        both("t2", B("t2", 0, 16), 16, B(p, 0, 16), kc, A.is_le, B(m, 0, 16), kc, A.is_gt, A.mult, (p, m, kct))
        for q in range(8):
            ts(16, B(name, 16 * q, 16 * q + 16), B("t2", 0, 16), B("bm", 16 * q, 16 * q + 1), A.mult, r=("t2", "bm"), w=(name if q == 7 else name + str(q),))
    r5, r5t = col(1, kc, 5.0, A.is_ge, 9000.0, A.mult, r=(kct,))
    zl, zlt = col(1, kc, 11.0, A.is_ge, -8997.0, A.mult, r=(kct,))
    lo, lot = col(1, r5, zl, A.add, r=(r5t, zlt))
    l1, l1t = col(1, lo, 1.0, A.add, r=(lot,))
    l2, l2t = col(1, lo, 2.0, A.add, r=(lot,))
    ts(128, B("t3"), B("jj"), l1, A.is_le, r=("jj", l1t), w=("t3",))
    ts(128, B("t2"), B("jj"), lo, A.is_ge, -1.0, A.mult, r=("jj", lot), w=("t2",))
    tt(128, B("wza"), B("t2"), B("t3"), A.mult, r=("t2", "t3"), w=("wza",))
    both("wzb", B("wzb"), 128, B("jj"), l1, A.is_ge, B("jj"), l2, A.is_le, A.mult, ("jj", l1t, l2t))

    def spread(name, terms):
        c = ct = None
        for co, t in terms:
            if c is None:
                c, ct = col(1, B("ek", t, t + 1), float(co), A.mult, r=("ek",))
            else:
                c, ct = col(1, B("ek", t, t + 1), float(co), A.mult, c, A.add, r=("ek", ct))
        ts(128, B(name), B("bm"), c, A.mult, r=("bm", ct), w=(name,))
    fn("f0", 0.0, ((1, 2), (2, 3), (1, 5), (99, 6)))
    fn("f1", 1.0, ((1, 1), (2, 3), (1, 4), (99, 6)))
    signs("wc", "f0", "f1")
    ts(8, B("wc", 15, 128, 16), B("bm", 15, 128, 16), B("ek", 15, 16), A.mult, 2.0, A.mult, r=("bm", "ek", "wc"), w=("wc",))
    spread("wl0", ((1, 0), (-1, 3)))
    spread("wl2", ((1, 2), (-1, 5)))
    for wname, cname, a0, p, m in (("wta", "ca", (5, 7), ((-5, 5), (-6, 11), (99, 15)), ((-6, 5), (-4, 11), (99, 15))),
                                   ("wtb", "cb", (99, 103), ((-99, 5), (-3, 8), (-2, 10), (99, 11)), ((-99, 5), (-2, 8), (-1, 10), (99, 11)))):
        for q, (dst, steps) in enumerate((("f2", p), ("f3", m))):
            fn(dst, None, steps)
            ts(17, B(dst), B(dst), float(a0[q]), A.add, r=(dst,), w=(dst,))
        window(wname, "f2", "f3")
        signs(cname, "f2", "f3")
    tE, tEt = col(1, ici[:, 2:3], 999.0, A.mult, r=("i2",))
    ta, tat = col(1, ici[:, 1:2], -1.0, A.mult, pc, A.add, r=("i1", pct))
    te, tet = col(1, ta, tE, A.add, 3.0, A.add, r=(tat, tEt))
    to, tot = col(1, tE, -1.0, A.mult, ta, A.add, r=(tEt, tat))
    to, tot = col(1, to, 16 * 999.0 + 3.0, A.add, r=(tot,))
    ts(131, B("ale"), B("ia", 0, 131), te, A.is_equal, kc, A.mult, r=("ia", tet, kct), w=("ale",))
    ts(131, B("alo"), B("ia", 0, 131), to, A.is_equal, kc, A.mult, r=("ia", tot, kct), w=("alo",))
    k16, k16t = col(1, kc, 16.0, A.mult, r=(kct,))
    cp(128, B("idh"), B("idf"), r=("idf",), w=("idh",))
    cp(128, B("ndh"), B("ndf"), r=("ndf",), w=("ndh",))
    ts(128, B("i4h"), B("idf"), 4096.0, A.mult, r=("idf",), w=("i4h",))
    k37, k37t = col(1, kc, 37.0, A.mult, r=(kct,))
    ts(128, B("d37"), B("idf"), k37, A.mult, r=("idf", k37t), w=("d37",))
    both("wr", B("wr"), 128, B("jj"), kc, A.is_ge, B("bm"), 1.0, A.mult, A.mult, ("jj", kct, "bm"))
    ts(128, B("wrn"), B("wr"), -1.0, A.mult, r=("wr",), w=("wrn",))
    fn("f4", None, ((-3, 3), (99, 6)))
    ts(128, B("wp2"), B("jj"), B("f4", 16, 17), A.is_equal, r=("jj", "f4"), w=("wp2",))
    spread("wsn", ((-1, 0), (-1, 1), (-1, 2)))
    spread("bl0", ((1, 0),))
    spread("bl2", ((1, 2),))
    spread("br0", ((1, 3), (-1, 15)))
    spread("br2", ((1, 5), (-1, 15)))
    spread("b2k", ((2048, 15),))
    cp(1, B("thf", 0, 1), T.thi[:], r=("thi",), w=("thf0",))

    for c in range(NC):
        for s in (2, 0, 3, 1):
            cp(64, T.off0[:, c * 256 + s * 64:c * 256 + s * 64 + 64], T.homi[:, s * 192 + c * 64:s * 192 + c * 64 + 64], r=("homi",), w=("off0_%d_%d" % (c, s),))

    def gather(v, c, s, h):
        lo = c * 256 + s * 64 + h * 32
        at = c * 1024 + h * HALF
        out, in_ = T["g%d" % s][:, at:at + HALF], T.xs[:, 0:4096].indirect(T["off%d" % v][:, lo:lo + 32])
        r, w = ("x0", "x1", "x2", "x3", "off%d_%d_%d" % (v, c, s)), ("g%d_%d_%d" % (s, c, h),)
        if c == 0 and (s, h) in DG:
            cp(0, out, in_, r=r, w=w, cost=60 + GAM * HALF)
        else:
            act(0, out, in_, F.Copy, r=r, w=w, cost=70 + GAM * HALF)
    uc = [0]

    def ufill(c, s, h):
        bank = uc[0] % 3
        uc[0] += 1
        at = c * 1024 + h * HALF
        mms(bank, 0, 512, [(B("idb"), T["g%d" % s][:, at:at + HALF], ("idb", "g%d_%d_%d" % (s, c, h)))])
        return bank

    def pair(c, par, s, bank, name, h):
        at = c * 1024 + h * HALF
        tt(HALF, T["d%s_%d" % (name, par)][:, h * HALF:h * HALF + HALF], T["g%d" % s][:, at:at + HALF], pb[bank][:, 0:512], A.max,
           r=("g%d_%d_%d" % (s, c, h),), w=("d%s_%d_%d" % (name, par, h),), b=(bank,))

    def red(par, name, bank, at, first, last):
        d = T["d%s_%d" % (name, par)]
        toks = ("red", "d%s_%d_0" % (name, par), "d%s_%d_1" % (name, par))
        for q in range(2):
            mms(bank, at, at + 64, [(B("red", 15 - k, 143 - k), d[:, k:1024:16], toks) for k in range(8 * q, 8 * q + 8)],
                first and q == 0, last and q == 1)

    def add_up(v, c):
        for j, (to_, s) in enumerate(((3, 2), (1, 0))):
            toks = ["g%d_%d_%d" % (z, c, h) for z in (s, to_) for h in range(2)]
            out, in_ = T["g%d" % to_][:, c * 1024:c * 1024 + 1024], T["g%d" % s][:, c * 1024:c * 1024 + 1024]
            op("pool", [(lambda o_, i_: lambda: g.dma_start(out=o_, in_=i_, accum_op=A.add))(out, in_)], 1000.0, toks, toks[2:],
               ext=("ds%d_%d_%d" % (v, c, j), 16), lat=3500.0)

    def total(c, bk):
        for q, s in enumerate((3, 1)):
            for e in range(2):
                mms(bk, 384, 448, [(B("reds", 15 - k, 143 - k), T["g%d" % s][:, c * 1024 + k:c * 1024 + 1024:16],
                                    ("reds", "g%d_%d_0" % (s, c), "g%d_%d_1" % (s, c))) for k in range(8 * e, 8 * e + 8)], q + e == 0, q + e == 2)

    def main(v, c):
        par = (v * NC + c) % 2
        u2 = [ufill(c, 2, 0), ufill(c, 2, 1)]
        pair(c, par, 0, u2[0], "02", 0)
        pair(c, par, 0, u2[1], "02", 1)
        red(par, "02", 4, 0, True, False)
        pair(c, par, 3, u2[0], "23", 0)
        pair(c, par, 3, u2[1], "23", 1)
        red(par, "23", 5, 0, True, False)
        u3 = [ufill(c, 3, 0)]
        pair(c, par, 0, u3[0], "03", 0)
        u3.append(ufill(c, 3, 1))
        pair(c, par, 0, u3[1], "03", 1)
        pair(c, par, 1, u3[0], "13", 0)
        pair(c, par, 1, u3[1], "13", 1)
        red(par, "13", 4, 0, False, True)
        u1 = [ufill(c, 1, 0)]
        pair(c, par, 0, u1[0], "01", 0)
        u1.append(ufill(c, 1, 1))
        pair(c, par, 0, u1[1], "01", 1)
        red(par, "01", 5, 0, False, True)
        m1 = "m1_%d" % c
        act(64, B(m1), pb[4][:, 0:64], F.Copy, w=(m1,), b=(4,))
        red(par, "03", 4, 64, True, False)
        tt(64, B("ab_%d" % c, 0, 64), pb[5][:, 0:64], B(m1), A.subtract, r=(m1,), w=("a_%d" % c,), b=(5,))
        pair(c, par, 2, u1[0], "12", 0)
        pair(c, par, 2, u1[1], "12", 1)
        red(par, "12", 4, 64, False, True)
        tt(64, B("ab_%d" % c, 64, 128), pb[4][:, 64:128], B(m1), A.subtract, r=(m1,), w=("b_%d" % c,), b=(4,))
        add_up(v, c)

    def crit(v, c):
        bk = 6
        n = lambda s: "%s_%d" % (s, c)
        mms(bk, 0, 64, [(B("wza"), B(n("ab"), 0, 64), ("wza", n("a"))), (B("wzb"), B(n("ab"), 64, 128), ("wzb", n("b")))])
        act(64, B(n("u")), pb[bk][:, 0:64], F.Sign, 0.5, w=(n("u"),), b=(bk,))
        mms(bk, 64, 128, [(B("wc"), B(n("u")), ("wc", n("u")))])
        act(64, B(n("o")), pb[bk][:, 64:128], F.Relu, -1.0, w=(n("o"),), b=(bk,))
        mms(bk, 128, 192, [(B("wl0"), B(n("o")), ("wl0", n("o")))])
        mms(bk, 192, 256, [(B("wl2"), B(n("o")), ("wl2", n("o")))])
        tt(128, B(n("y")), B(n("ab")), pb[bk][:, 128:256], A.mult, r=(n("a"), n("b")), w=(n("y"),), b=(bk,))
        for q, m in enumerate(("wta", "wtb")):
            mt = tuple([m] + [m + str(e) for e in range(7)])
            mms(bk, 256 + 64 * q, 320 + 64 * q, [(B(m), B(n("y"), 0, 64), mt + (n("y"),)), (B(m), B(n("y"), 64, 128), mt + (n("y"),))])
        act(128, B(n("tu")), pb[bk][:, 256:384], F.Sign, 0.5, w=(n("tu"),), b=(bk,))
        mms(bk, 384, 448, [(B("ca"), B(n("tu"), 0, 64), ("ca", n("tu"))), (B("cb"), B(n("tu"), 64, 128), ("cb", n("tu")))])
        act(64, B(n("om")), pb[bk][:, 384:448], F.Relu, -5.0, w=(n("om"),), b=(bk,))
        for q, m in enumerate(("ale", "alo")):
            mms(bk, 448 + 16 * q, 464 + 16 * q, [(B("rw")[0:1, :], B("onb", 0, 16)[0:1, :], ("rw", "onb"))] +
                [(B(m, 3 - r, 131 - r), B(n("om"), 16 * r, 16 * r + 16), (m, n("om"))) for r in range(4)])
        op("dve", [lambda: g.vector.transpose(out=B(n("lt")), in_=pb[bk][:, 448:480])], 64, (), (n("lt"),), (bk,))
        li, lit = T.lists[:, 4 * c:4 * c + 4], n("li")
        ts(4, li, B(n("lt"), 0, 4), k16, A.add, r=(n("lt"), k16t), w=(lit,))
        gr = (lit, "g0_%d_0" % c, "g0_%d_1" % c)
        if c < NC - 1:
            act(64, B(n("gs")), T.g0[:, c * 1024:c * 1024 + 1024].indirect(li), F.Copy, r=gr, w=(n("gs"),), cost=75 + 64 * GAM)
        else:
            cp(64, B(n("gs")), T.g0[:, c * 1024:c * 1024 + 1024].indirect(li), r=gr, w=(n("gs"),), cost=60 + 64 * GAM)
        tt(64, B(n("ts")), T.xs[:, c * 1024:c * 1024 + 1024].indirect(li), B(n("gs")), A.add, r=(lit, n("gs"), "x%d" % c), w=(n("ts"),), cost=60 + 64 * GAM)
        ts(64, B(n("tq")), B(n("ts")), 0.5, A.mult, 191.75, A.add, r=(n("ts"),), w=(n("tq"),))

    def scatter(c):
        tt(64, T.xs[:, c * 1024:c * 1024 + 1024].indirect(T.lists[:, 4 * c:4 * c + 4]), B("tq_%d" % c), B("m192"), A.add,
           r=("tq_%d" % c, "m192", "li_%d" % c), w=("x%d" % c,), cost=60 + 64 * SCA)

    def upd(v, c):
        bk, bz = 7, 3
        n = lambda s: "%s_%d" % (s, c)
        st, stt = B(n("st")), n("st")
        i16, n16, ib = B("idh"), B("ndh"), B("idb")
        ts(256, st, T["off%d" % v][:, c * 256:c * 256 + 256], -2048.0, A.add, r=tuple("off%d_%d_%d" % (v, c, s) for s in range(4)), w=(stt,))
        mms(bz, 448, 512, [(B("wp2"), B(n("o")), ("wp2", n("o")))])
        act(64, B(n("same")), pb[bz][:, 448:512], F.Relu, -1.0, accum=B("acc", c, c + 1), w=(n("same"), "acc%d" % c), b=(bz,))
        o, om = B(n("o")), B(n("om"))
        for q, (m, w) in enumerate((("bl0", "wrn"), ("br0", "wr"), ("bl2", "wrn"), ("br2", "wr"))):
            mms(bk, 64 * q, 64 * q + 64, [(B(m), o, (m, n("o"))), (B(w), om, (w, n("om")))])
        mms(bk, 256, 320, [(B("wr"), om, ("wr", n("om"))), (B("wsn"), B(n("same")), ("wsn", n("same")))])
        xr = n("xr")
        act(320, B(xr), pb[bk][:, 0:320], F.Relu, w=(xr,), b=(bk,))
        for q in range(4):
            a = q // 2 * 128
            mms(bz, 64 * q, 64 * q + 64, [(ib, B(xr, a, a + 64), ("idb", xr)), (ib, B(xr, a + 64, a + 128), ("idb", xr))])
        fs = n("fs")
        total(c, 5)
        tt(64, B(n("c1")), B(n("m1")), pb[5][:, 384:448], A.subtract, r=(n("m1"),), w=(n("c1"),), b=(5,))
        tt(128, B(fs, 0, 128), B(stt, 64, 192), pb[bz][:, 0:128], A.mult, r=(stt,), w=(fs,), b=(bz,))
        tt(128, B(fs, 128, 256), B(stt, 128, 256), pb[bz][:, 128:256], A.mult, r=(stt,), w=(fs + "x",), b=(bz,))
        tt(128, B(n("zz")), B(n("ab")), pb[bz][:, 64:192], A.mult, r=(n("a"), n("b")), w=(n("zz"),), b=(bz,))
        act(128, B(n("fb")), pb[bz][:, 64:192], F.Copy, w=(n("fb"),), b=(bz,))
        mms(5, 384, 448, [(i16, B(n("c1")), ("idh", n("c1"))), (i16, B(n("zz"), 0, 64), ("idh", n("zz"))), (i16, B(n("zz"), 64, 128), ("idh", n("zz")))])
        ts(64, B(n("vv")), pb[5][:, 384:448], B("thf", v % 2, v % 2 + 1), A.is_gt, r=("thf%d" % (v % 2),), w=(n("vv"),), b=(5,))
        f1, f2, h2, h3 = B(fs, 0, 64), B(fs, 64, 128), B(fs, 128, 192), B(fs, 192, 256)
        s0, s1, s2, s3 = [B(stt, 64 * q, 64 * q + 64) for q in range(4)]
        FT = ("idh", "ndh", stt, fs, fs + "x")
        mms(bk, 320, 384, [(i16, s1, FT), (n16, f1, FT), (i16, f2, FT)])
        cp(64, B(n("src"), 0, 64), pb[bk][:, 320:384], w=(n("src"),), b=(bk,))
        k2 = (B("b2k"), o, ("b2k", n("o")))
        qt = [(i16, s2, FT), (i16, f1, FT), (n16, f2, FT), (i16, h3, FT), (n16, h2, FT), k2]
        tq = [(i16, s3, FT), (n16, h3, FT), (i16, h2, FT), k2]
        mms(bk, 0, 64, qt)
        mms(bk, 64, 128, tq)
        vv = (B(n("vv")), ("idh", "d37", n("vv")))
        v4 = (B("i4h"), B(n("vv")), ("i4h", n("vv")))
        mms(bz, 128, 192, [(i16, s0, FT), v4])
        mms(bz, 192, 256, [(i16, B(n("src"), 0, 64), ("idh", n("src"))), v4])
        act(128, B(n("sr")), pb[bz][:, 128:256], F.Relu, b=(bz,), bias=-2048.0, w=(n("sr"),))
        mms(bz, 256, 320, qt + [(B("d37"),) + vv])
        mms(bz, 320, 384, tq + [(B("d37"),) + vv])
        tt(128, B(n("pp")), B(n("sr")), pb[bk][:, 0:128], A.mult, r=(n("sr"),), w=(n("pp"),), b=(bk,))
        ts(128, B(n("qq")), B(n("pp")), 5, A.arith_shift_right, r=(n("pp"),), w=(n("qq"),))
        tt(128, B(n("ui")), B(n("qq")), pb[bz][:, 256:384], A.add, r=(n("qq"),), w=(n("ui"),), b=(bz,))
        for q in range(3):
            mms(bk, 64 * q, 64 * q + 64, [(ib, B(xr, 256, 320), ("idb", xr))])
        ts(128, B(n("nb")), B(n("ui")), 4095, A.bitwise_and, r=(n("ui"),), w=(n("nb"),))
        ps = n("ps")
        ts(128, B(n("src"), 64, 192), B(n("nb")), -2048.0, A.add, r=(n("nb"),), w=(n("src") + "x",))
        tt(64, B(ps, 0, 64), s0, pb[bk][:, 0:64], A.mult, r=(stt,), w=(ps,), b=(bk,))
        tt(192, B(ps, 64, 256), B(n("src")), pb[bk][:, 0:192], A.mult, r=(n("src"), n("src") + "x"), w=(ps + "x",), b=(bk,))
        r0, a1, b1 = [B(n("src"), 64 * q, 64 * q + 64) for q in range(3)]
        e0, er, ea, eb = [B(ps, 64 * q, 64 * q + 64) for q in range(4)]
        gd = n("gd")
        SX = ["idh", "ndh", n("src"), n("src") + "x", ps, ps + "x", stt]
        pos = lambda x: (i16, x, tuple(SX))
        neg = lambda x: (n16, x, tuple(SX))
        nq, nr, nt = [pos(a1), neg(ea), pos(e0)], [pos(r0), neg(er), pos(eb)], [pos(b1), neg(eb), pos(er)]
        mms(bz, 192, 256, nq)
        mms(bz, 256, 320, nr)
        mms(bz, 320, 384, nt)
        tt(64, B(gd, 0, 64), B(n("fb"), 0, 64), pb[bz][:, 192:256], A.mult, r=(n("fb"),), w=(gd,), b=(bz,))
        tt(64, B(gd, 64, 128), B(n("fb"), 64, 128), pb[bz][:, 192:256], A.mult, r=(n("fb"),), w=(gd + "x",), b=(bz,))
        tt(128, B(gd, 128, 256), B(n("fb")), pb[bz][:, 256:384], A.mult, r=(n("fb"),), w=(gd + "y",), b=(bz,))
        SX += [gd, gd + "x", gd + "y"]
        q1, q3, p1, p3 = [B(gd, 64 * q, 64 * q + 64) for q in range(4)]
        mms(bk, 0, 64, [pos(s0), neg(e0), pos(ea)])
        mms(bk, 64, 128, nr + [neg(p1), pos(q1)])
        mms(bk, 128, 192, nq + [neg(q1), pos(p1), neg(q3), pos(p3)])
        mms(bk, 192, 256, nt + [neg(p3), pos(q3)])
        snd, sdt = T["snd%d" % v], "snd%d_%d" % (v, c)
        if v < VI - 1:
            ts(192, snd[:, c * 192:c * 192 + 192], pb[bk][:, 64:256], 2048.0, A.add, w=(sdt,), b=(bk,))
            nxt = "off%d" % (v + 1)
            ts(64, T[nxt][:, c * 256:c * 256 + 64], pb[bk][:, 0:64], 2048.0, A.add, w=("%s_%d_0" % (nxt, c),), b=(bk,))
        else:
            act(192, snd[:, c * 192:c * 192 + 192], pb[bk][:, 64:256], F.Identity, 2048.0, w=(sdt,), b=(bk,))
            act(64, T.ysb[:, c * 64:c * 64 + 64], pb[bk][:, 0:64], F.Identity, 2048.0, w=("off%d_%d_0" % (VI, c),), b=(bk,))
        tr = []
        for s in (1, 2, 3):
            dst = T.cores[(rank + STEP[s]) % len(T.cores)]
            rid, pid, _ = topo.addr(dst)
            e = topo.engines(core, dst)
            if v < VI - 1:
                land = T["off%d" % (v + 1)][:, c * 256 + s * 64:c * 256 + s * 64 + 64]
            else:
                land = T.ysb[:, s * 192 + c * 64:s * 192 + c * 64 + 64]
            tr.append(RemoteDMATransfer(dst_ids=[DstId(rid=rid, pnc=pid)], dma_engine_mask=(1 << e[2 * s - 2]) | (1 << e[2 * s - 1]),
                                        remote_sem=T.sem["arr%d_%d" % (v, c)], src=snd[:, (c * 3 + s - 1) * 64:(c * 3 + s) * 64], dst=land))
        op("pool", [lambda: g.remote_dma_fused(tr, local_sem=T.sem.sent)], 1000.0, (sdt,), ("go",), ext="send")
        op(None, [], 0.0, ("go",), tuple("off%d_%d_%d" % (v + 1, c, s) for s in (1, 2, 3)), ext=("arr%d_%d" % (v, c), 6), lat=NET)
        if c == NC - 1 and v < VI - 1:
            cp(4, T.accb[:, 0:3], B("acc", 0, 3), r=("acc0", "acc1", "acc2"), w=("accb",))
            mms(bk, 0, 1, [(B("wsn"), T.accb[:, q:q + 1], ("wsn", "accb")) for q in range(3)])
            cp(1, ici[:, 3:4], pb[bk][:, 0:1], w=("i3",), b=(bk,))
            ts(1, ici[:, 4:5], ici[:, 3:4], 31, A.bitwise_and, r=("i3",), w=("i4",))
            w = (v + 1) % 2
            tt(1, B("thf", w, w + 1), ici[:, 4:5], T.thi[:], A.add, r=("i4", "thi"), w=("thf%d" % w,))

    for v in range(VI):
        for c in range(NC):
            lab[0] = "g%d" % c
            for s, h in GORDER:
                gather(v, c, s, h)
        for c in range(NC):
            lab[0] = "m%d" % c
            main(v, c)
            lab[0] = "c%d" % c
            crit(v, c)
            scatter(c)
            lab[0] = "u%d" % c
            if v == VI - 1:
                dma("sp", g.sync, T.yx[:, 1024 * c:1024 * c + 1024], T.xs[:, 1024 * c:1024 * c + 1024], ("dy0", "dy1", "dy3")[c], ("x%d" % c,))
            upd(v, c)
        if v == 0:
            dma("sp", g.sync, T.yx[:, 3072:4096], T.xs[:, 3072:4096], "dy2", ("x3",))
    dma("sp", g.sync, T.ys[:], T.ysb[:], "dys", tuple("off%d_%d_%d" % (VI, c, s) for c in range(NC) for s in range(4)))

    if "order" not in CACHE:
        CACHE["order"] = schedule(nodes)
    known = {q: {} for q in Q}
    cnt = {q: 0 for q in Q}
    snap, ident, seen = {}, {}, set()

    def wait(q, deps):
        todo = sorted({d for d in deps if known[q].get(d[0], 0) < d[1]}, key=lambda d: (-len(snap.get(d, {})), d[0], -d[1]))
        for s, k in todo:
            if known[q].get(s, 0) >= k:
                continue
            Q[q].wait_ge(T.sem[s], k)
            seen.add((s, k))
            known[q][s] = k
            for s2, k2 in snap.get((s, k), {}).items():
                if known[q].get(s2, 0) < k2:
                    known[q][s2] = k2
    sent = 0
    for i in CACHE["order"]:
        x = nodes[i]
        q = x["q"]
        if q is None:
            ident[i] = x["ext"]
            continue
        wait(q, [ident[d] for d in x["deps"] if d in ident])
        for f in x["fns"]:
            ins = f()
            if x["ext"] is None:
                cnt[q] += 1
                ident[i] = ("s_" + q, cnt[q])
                ins.then_inc(T.sem["s_" + q], 1)
            elif x["ext"] == "send":
                sent += 6
            else:
                ident[i] = x["ext"]
                ins.then_inc(T.sem[x["ext"][0]], 16)
        if i in ident:
            snap[ident[i]] = dict(known[q])
    ends = [("s_" + q, cnt[q]) for q in ("pe", "dve", "act", "pool")] + [("sent", sent)]
    ends += [(s, 6 if s[:3] == "arr" else 16) for s in SEMAPHORES if s[:2] != "s_" and s != "sent"]
    known["pool"].clear()
    snap.clear()
    wait("pool", [e for e in ends if e not in seen])
